import numpy as np, ml_dtypes
CORES = [6,15,38,47]
N = 4
BF = ml_dtypes.bfloat16
A, W, B, BL, RO = 512, 4096, 128, 1, 4
def parts(rng):
    share = rng.choice(np.array([0.5, 0.75, 0.95]), (N, 8, 1, 1)) * rng.random((N, 8, 1, A))
    s = np.where(rng.random((N, 8, 16, A)) < share, 4096, rng.integers(0, 4096, (N, 8, 16, A)))
    l = np.minimum(np.maximum(rng.integers(90, 201, (N, 8, 1, A)) + rng.integers(-60, 61, (N, 8, 16, A)), 0), 255)
    return s, l, rng.integers(0, 4096, (N, 8, A)), rng.integers(0, 256, (N, 8, 16, W))
def pack(s, l, k, f):
    return {"sr": np.ascontiguousarray(s.reshape(N, 128, A)).astype(np.int32), "lim": np.ascontiguousarray(l.reshape(N, 128, A)).astype(np.int32),
            "u": np.ascontiguousarray(k).astype(np.int32), "fit": np.ascontiguousarray(f.reshape(N, 128, W)).astype(np.float32).astype(BF)}
def setup_inputs(rng):
    return pack(*parts(rng))
def setup_inputs_ties(rng):
    s, l, k, f = parts(rng); g = rng.permutation(8); cnt = rng.integers(0, 17, (N, 8, A))
    cnt[:, g[0]] = rng.integers(15, 17, (N, A)); cnt[:, g[1]] = rng.choice(np.array([0, 15, 16]), (N, A)); cnt[:, g[2]] = 8
    cnt[:, g[3]] = 0; cnt[:, g[4]] = 16; cnt[:, g[4], 0] = 0; cnt[:, g[4], A - 1] = 0
    cnt[:, g[5]] = 0
    for q in rng.permutation(N)[1:]: cnt[q, g[5], rng.permutation(A // 2)[:A // 32]] = 1
    l[:, g[[0, 1, 2, 5]]] = 255
    whole = rng.integers(0, 4096, s.shape)
    s = np.where(np.argsort(rng.random(s.shape), axis=2) < cnt[:, :, None, :], 4096, whole)
    return pack(s, l, k, f)
def setup_inputs_level(rng):
    s, l, k, f = parts(rng); base = rng.integers(1, 255, (1, 8, 16, 1))
    n = rng.choice(np.array([0, 3, 5, 7, 7, 8, 8, 11, 11, 12]), (N, 8, 1, W))
    over = np.argsort(rng.random(f.shape, dtype=np.float32), axis=2) < n
    f = base + np.where(over, 1, -rng.integers(0, 2, f.shape))
    return pack(s, l * 0 + base, k, f)
def setup_inputs_ends(rng):
    s, l, k, f = parts(rng); g = rng.permutation(8)
    e = rng.choice(np.array([0, 1, 31, 32, 2048, 4094, 4095]), s.shape)
    s = np.where((s < 4096) & (rng.random((N, 8, 1, A)) < 0.7), e, s)
    k = np.where(rng.random(k.shape) < 0.7, rng.choice(np.array([0, 1, 31, 32, 2048, 4094, 4095, 3099, 2102, 1105]), k.shape), k)
    m = rng.integers(0, 6, (N, 8, 1, A))
    l = np.where(m == 0, 0, np.where(m == 1, 255, np.where(m == 2, 255 * rng.integers(0, 2, l.shape), l)))
    f[:, g[:4]] = 255 * rng.integers(0, 2, (N, 4, 16, W))
    f[:, :, :, 0] = 255 * rng.integers(0, 2, (N, 8, 16)); f[:, :, :, W - 1] = 255 * rng.integers(0, 2, (N, 8, 16))
    q = int(rng.integers(0, N)); hole = (np.argsort(rng.random((8, 16, 1)), axis=1) < 8) == (np.arange(A) < A // 2)
    s[q] = np.where(hole, 4096, np.where(rng.random(hole.shape) < 0.7, e[q], rng.integers(0, 4096, hole.shape))); l[q] = 255
    return pack(s, l, k, f)
def setup_inputs_alike(rng):
    s, l, k, f = parts(rng); o = rng.permutation(8); g = o[:4]; d = int(o[4]); q = rng.permutation(N)
    s[q[0]] = rng.integers(0, 4096, (8, 16, A)); s[q[1]] = np.where(rng.random((8, 16, A)) < 0.9, 4096, rng.integers(0, 4096, (8, 16, A)))
    for h in g:
        few = rng.integers(0, 4096, 5); s[:, h] = np.where(s[:, h] < 4096, few[rng.integers(0, 5, (N, 16, A))], 4096)
        k[:, h] = int(rng.integers(0, 4096))
    f[:, d] = f[:, d] % 101; f[q[0], d] = rng.integers(200, 256, (16, W)); l[q[0], d] = rng.integers(100, 200, (16, A))
    return pack(s, l, k, f)
def setup_inputs_spread(rng):
    s, l, k, f = parts(rng)
    s = np.where(s < 4096, np.minimum(np.exp2(12 * rng.random(s.shape)).astype(np.int64), 4095), 4096)
    k = np.minimum(np.exp2(12 * rng.random(k.shape)).astype(np.int64), 4095)
    l = np.minimum((np.exp2(4 + 4 * rng.random((N, 8, 1, A))) * (0.5 + 0.5 * rng.random(l.shape))).astype(np.int64), 255)
    f = np.minimum((np.exp2(8 * rng.random((N, 8, 1, W))) * rng.random(f.shape)).astype(np.int64), 255)
    return pack(s, l, k, f)
def check_inputs(d):
    bad = []
    for n, hi in (("sr", 4096), ("lim", 255), ("u", 4095), ("fit", 255)):
        a = np.asarray(d[n]).astype(np.float64)
        if not (np.min(a) >= 0 and np.max(a) <= hi): bad.append("range of " + n)
    a = np.asarray(d["fit"]).astype(np.float32)
    if not np.all(a == np.floor(a)): bad.append("whole numbers in fit")
    return bad
def records(f, s, v):
    c = ((s * v[:, :, None, :]) >> 5) & (W - 1)
    return np.take_along_axis(f, c.reshape(N, 8, 1, -1), 3).reshape(N, 8, 16, 16, -1)
def reference(sr, lim, u, fit):
    s = sr.astype(np.int64).reshape(N, 8, 16, A); l = lim.astype(np.int16).reshape(N, 8, 16, A); k = u.astype(np.int64)
    f = fit.astype(np.float32).astype(np.int16).reshape(N, 8, 16, W); h = A // 2
    for t in range(RO):
        over = np.sum(records(f, s, (k + 997 * t) & 4095) > l[:, :, :, None, :], axis=2)
        s = np.where(over >= 12, 4096, s)
        holes = np.minimum(np.sum(s == 4096, axis=2), 15)
        o = np.argsort(holes, axis=2, kind="stable")
        s = np.take_along_axis(s, o[:, :, None, :], 3); l = np.take_along_axis(l, o[:, :, None, :], 3); k = np.take_along_axis(k, o, 2)
        have = s[..., :h]; give = s[..., h:][..., ::-1]
        good = np.sum(records(f, give, (k[..., :h] + 997 * t) & 4095) <= l[:, :, :, None, :h], axis=2)
        move = (have == 4096) & (give < 4096) & (good >= 9)
        s = np.concatenate([np.where(move, give, have), np.where(move, 4096, give)[..., ::-1]], axis=3)
        for b in range(BL):
            c = slice(A - BL * B + b * B, A - BL * B + (b + 1) * B)
            s[..., c] = np.roll(s[..., c], b + 1, axis=0); l[..., c] = np.roll(l[..., c], b + 1, axis=0); k[..., c] = np.roll(k[..., c], b + 1, axis=0)
    return {"ysr": s.reshape(N, 128, A).astype(np.float32), "ylim": l.reshape(N, 128, A).astype(np.float32), "yu": k.astype(np.float32)}

@@ -1,0 +1,640 @@
+from concourse.mybir import AluOpType as A, AxisListType, ActivationFunctionType as F
+
+SCRATCH = {
+    "FITW": ("sbuf", [128, 4096], "bfloat16"), "SRI": ("sbuf", [128, 512], "int32"), "LMI": ("sbuf", [128, 512], "int32"),
+    "U8": ("sbuf", [8, 512], "int32"), "U16": ("sbuf", [8, 512], "float16"), "K8": ("sbuf", [8, 512], "bfloat16"),
+    "E8A": ("sbuf", [8, 128], "bfloat16"), "E8": ("sbuf", [8, 128], "bfloat16"),
+    "ON": ("sbuf", [128, 512], "bfloat16"), "ID": ("sbuf", [128, 128], "bfloat16"),
+    "BLA": ("sbuf", [128, 128], "bfloat16"), "BLK": ("sbuf", [128, 128], "bfloat16"),
+    "G8A": ("sbuf", [128, 8], "bfloat16"), "G8": ("sbuf", [128, 8], "bfloat16"), "LJ": ("sbuf", [128, 2048], "bfloat16"),
+    "IOT": ("sbuf", [128, 512], "bfloat16"), "BI": ("sbuf", [128, 2], "int32"), "BJ": ("sbuf", [128, 2], "int32"),
+    "BCF": ("sbuf", [128, 1], "float32"), "BCH": ("sbuf", [128, 1], "float32"),
+    "JI": ("sbuf", [128, 16], "float32"), "M16": ("sbuf", [128, 16], "float32"), "TB": ("sbuf", [128, 144], "float32"),
+    "TM": ("sbuf", [128, 96], "float32"), "COL": ("sbuf", [128, 8], "float32"), "W08": ("sbuf", [128, 8], "float16"),
+    "R1": ("sbuf", [128, 8], "int32"), "R2": ("sbuf", [128, 8], "int32"), "R3": ("sbuf", [128, 8], "int32"),
+    "R4": ("sbuf", [128, 8], "int32"), "RL": ("sbuf", [128, 8], "uint16"),
+    "KI": ("sbuf", [128, 512], "int32"), "KJ": ("sbuf", [128, 512], "int32"),
+    "S0": ("sbuf", [128, 512], "float32"), "SW": ("sbuf", [128, 512], "float32"), "SN": ("sbuf", [128, 256], "float32"),
+    "SGV": ("sbuf", [128, 256], "float32"), "FN": ("sbuf", [128, 256], "bfloat16"), "WB": ("sbuf", [128, 256], "bfloat16"),
+    "FL": ("sbuf", [128, 512], "bfloat16"), "CI": ("sbuf", [128, 512], "int32"), "CJ": ("sbuf", [128, 512], "int32"),
+    "CRI": ("sbuf", [128, 256], "int32"), "CRJ": ("sbuf", [128, 256], "int32"),
+    "CK": ("sbuf", [128, 512], "uint16"), "CR": ("sbuf", [128, 256], "uint16"),
+    "LX": ("sbuf", [128, 8192], "bfloat16"), "CM": ("sbuf", [128, 8192], "bfloat16"), "CMR": ("sbuf", [128, 4096], "bfloat16"),
+    "RS": ("sbuf", [128, 8192], "bfloat16"), "SG": ("sbuf", [128, 8192], "bfloat16"),
+    "HH": ("sbuf", [128, 512], "bfloat16"), "OH": ("sbuf", [128, 512], "bfloat16"), "JUNK": ("sbuf", [128, 512], "bfloat16"),
+    "ACC": ("sbuf", [128, 1], "float32"), "VAL": ("sbuf", [128, 512], "bfloat16"), "PR": ("sbuf", [128, 512], "bfloat16"),
+    "PL": ("sbuf", [128, 32], "uint16"), "OI": ("sbuf", [128, 512], "bfloat16"), "OL": ("sbuf", [128, 32], "uint16"),
+    "DFL": ("sbuf", [128, 128], "float32"), "DF": ("sbuf", [128, 128], "float32"),
+    "YL": ("sbuf", [128, 512], "float32"), "YU": ("sbuf", [8, 512], "float32"),
+}
+for _w in ("N8", "P8", "N16", "P16", "M256", "NEG", "P4096"):
+    SCRATCH["I_" + _w] = ("sbuf", [128, 128], "bfloat16")
+for _t in range(4):
+    SCRATCH["WT%d" % _t] = ("sbuf", [128, 128], "float16")
+    SCRATCH["SO%d" % _t] = ("sbuf", [128, 512], "float32")
+    SCRATCH["AR%d" % _t] = ("sbuf", [128, 128], "float32")
+    SCRATCH["AW%d" % _t] = ("sbuf", [128, 128], "bfloat16")
+    SCRATCH["KL%d" % _t] = ("sbuf", [128, 128], "bfloat16")
+    SCRATCH["LL%d" % _t] = ("sbuf", [128, 128], "bfloat16")
+    SCRATCH["WRV%d" % _t] = ("sbuf", [128, 256], "bfloat16")
+for _t in range(5):
+    SCRATCH["KB%d" % _t] = ("sbuf", [128, 512], "bfloat16")
+    SCRATCH["LW%d" % _t] = ("sbuf", [128, 512], "bfloat16")
+BANKS = ["D0", "D1", "OVV", "OVS", "GDA", "VA", "VB", "VC"]
+for _b in BANKS:
+    SCRATCH[_b] = ("psum", [128, 512], "float32")
+SEMAPHORES = ["qV", "qS", "qT", "qG", "ldu", "lds", "ldl", "ldf", "outs", "rloc"]
+SEMAPHORES += ["r%s%d" % (_k, _t) for _k in "sklw" for _t in range(4)]
+
+CYC = 0.00083
+GV, GS, SGN = 1.5 * CYC, 1.5 * CYC, 1.0 * CYC
+VI = 288
+VR, V3 = 220, 160
+
+
+def rank_program(g, core, T, topo):
+    rank = T.rank_of(core)
+    if rank is None:
+        return
+    nxt = T.cores[(rank + 1) % len(T.cores)]
+    assert topo.may_write(core, nxt)
+    rid, pid = topo.addr(nxt)[:2]
+    rmask = topo.mask(core, nxt)
+    reng = len(topo.engines(core, nxt))
+    Q = {"V": g.vector, "S": g.scalar, "T": g.tensor, "G": g, "Y": g.sync}
+    cnt = {e: 0 for e in Q}
+    known = {e: {} for e in Q}
+    snaps = {}
+    acc = {}
+    ps = {b: ({}, {}) for b in BANKS}
+    remote_total = [0]
+
+    def wait(e, need):
+        for s in sorted(need, key=lambda s: -len(snaps.get((s, need[s]), {}))):
+            v = need[s]
+            if known[e].get(s, 0) >= v:
+                continue
+            Q[e].wait_ge(T.sem[s], v)
+            known[e][s] = v
+            for s2, v2 in snaps.get((s, v), {}).items():
+                if known[e].get(s2, 0) < v2:
+                    known[e][s2] = v2
+
+    def deps(e, R, W):
+        need = {}
+
+        def add(tok):
+            if need.get(tok[0], 0) < tok[1]:
+                need[tok[0]] = tok[1]
+        for (b, lo, hi), w in [(x, False) for x in R] + [(x, True) for x in W]:
+            if b in ps:
+                anyd, wd = ps[b]
+                for e2, c in anyd.items():
+                    if e2 != e:
+                        add(("q" + e2, c))
+                if not w and e in wd:
+                    add(("q" + e, wd[e]))
+                continue
+            for r in acc.get(b, ()):
+                if r[0] < hi and lo < r[1]:
+                    if not w and r[4]:
+                        add(r[3])
+                    elif w and r[2] != e:
+                        add(r[3])
+        return need
+
+    def note(e, tok, R, W):
+        for (b, lo, hi), w in [(x, False) for x in R] + [(x, True) for x in W]:
+            if b in ps:
+                ps[b][0][e] = tok[1]
+                if w:
+                    ps[b][1][e] = tok[1]
+                continue
+            L = acc.setdefault(b, [])
+            if w:
+                L[:] = [r for r in L if not (lo <= r[0] and r[1] <= hi)]
+            else:
+                L[:] = [r for r in L if not (not r[4] and r[2] == e and lo <= r[0] and r[1] <= hi)]
+            L.append((lo, hi, e, tok, w))
+
+    def op(e, fn, R=(), W=()):
+        wait(e, deps(e, R, W))
+        ins = fn(Q[e])
+        cnt[e] += 1
+        s = "q" + e
+        ins.then_inc(T.sem[s], 1)
+        snaps[(s, cnt[e])] = dict(known[e])
+        note(e, (s, cnt[e]), R, W)
+
+    def load(q, out, src, sem, buf, n):
+        Q[q].dma_start(out, src).then_inc(T.sem[sem], 16)
+        acc.setdefault(buf, []).append((0, n, "D", (sem, 16), True))
+
+    def P(b, lo, hi, n=128):
+        return T[b][0:n, lo:hi] if n < 128 else T[b][:, lo:hi]
+
+    def cp(o, i):
+        op("V", lambda q: q.tensor_copy(P(*o), P(*i)), [i], [o])
+
+    def tt(o, a, b, f):
+        op("V", lambda q: q.tensor_tensor(P(*o), P(*a), P(*b), f), [a, b], [o])
+
+    def ts(o, a, s1, f1, s2=None, f2=None, n=128):
+        R = [a]
+        v1, v2 = s1, s2
+        if isinstance(s1, tuple):
+            R.append(s1)
+            v1 = P(*s1)
+        if isinstance(s2, tuple):
+            R.append(s2)
+            v2 = P(*s2)
+        if f2 is None:
+            op("V", lambda q: q.tensor_scalar(P(*o, n), P(*a, n), v1, None, f1), R, [o])
+        else:
+            op("V", lambda q: q.tensor_scalar(P(*o, n), P(*a, n), v1, v2, f1, f2), R, [o])
+
+    def vgather(o, win, off):
+        op("V", lambda q: q.tensor_copy(P(*o), P(*win).indirect(P(*off))), [win, off], [o])
+
+    def sgather(o, win, off):
+        op("S", lambda q: q.activation(P(*o), P(*win).indirect(P(*off)), F.Copy), [win, off], [o])
+
+    def act(o, i, f, bias=0.0, scale=1.0, n=128):
+        if f == F.Copy:
+            op("S", lambda q: q.activation(P(*o, n), P(*i, n), f, scale=scale), [i], [o])
+        else:
+            op("S", lambda q: q.activation(P(*o, n), P(*i, n), f, bias=bias, scale=scale), [i], [o])
+
+    def mm(o, lhs, rhs, start, stop, step=None, kn=128, mn=128):
+        def f(q):
+            r = T[rhs[0]][0:kn, rhs[1]:rhs[2]:step] if step else P(*rhs, kn)
+            return q.matmul(P(*o, mn), P(*lhs, kn), r, start, stop)
+        op("T", f, [lhs, rhs], [o])
+
+    def lj(i):
+        return ("LJ", i * 128, i * 128 + 128)
+
+    def full(b):
+        return (b, 0, 128)
+
+    FW = ("FITW", 0, 4096)
+
+    load("Y", T.U8[:], T.u[:], "ldu", "U8", 512)
+    load("Y", T.SRI[:], T.sr[:], "lds", "SRI", 512)
+    load("Y", T.LMI[:], T.lim[:], "ldl", "LMI", 512)
+    load("S", T.FITW[:], T.fit[:], "ldf", "FITW", 4096)
+
+    def sel(o, i, pat, cmp, base, cm, n=128):
+        op("G", lambda q: q.affine_select(P(*o, n), P(*i, n), pat, cmp, 0.0, base, cm), [i], [o])
+
+    def fill(o, v, n=128):
+        op("V", lambda q: q.memset(P(*o, n), v), [], [o])
+    fill(("ON", 0, 512), 1.0)
+    fill(("K8", 0, 512), 256.0, 8)
+    fill(("LJ", 0, 2048), 0.0)
+    sel(("E8A", 0, 128), ("ON", 0, 128), [[1, 128]], A.is_ge, 0, -16, 8)
+    sel(("E8", 0, 128), ("E8A", 0, 128), [[-1, 128]], A.is_ge, 15, 16, 8)
+    op("G", lambda q: q.iota(T.BI[:, 0:2], [[0, 2]], 0, 1), [], [("BI", 0, 2)])
+    op("G", lambda q: q.iota(T.JI[:], [[1, 16]], 0, 0, allow_small_or_imprecise_dtypes=True), [], [("JI", 0, 16)])
+    sel(("G8A", 0, 8), ("ON", 0, 8), [[-16, 8]], A.is_ge, 0, 1)
+    sel(("G8", 0, 8), ("G8A", 0, 8), [[16, 8]], A.is_ge, 15, -1)
+    sel(full("ID"), ("ON", 0, 128), [[-1, 128]], A.is_equal, 0, 1)
+    sel(full("BLA"), ("ON", 0, 128), [[-16, 8], [0, 16]], A.is_ge, 0, 1)
+    sel(full("BLK"), full("BLA"), [[16, 8], [0, 16]], A.is_ge, 15, -1)
+    op("G", lambda q: q.iota(T.R1[:], [[0, 8]], 127, -1), [], [("R1", 0, 8)])
+    op("G", lambda q: q.iota(T.R2[:], [[-16, 8]], 112, 0), [], [("R2", 0, 8)])
+    op("G", lambda q: q.iota(T.IOT[:], [[1, 512]], -256, 0, allow_small_or_imprecise_dtypes=True), [], [("IOT", 0, 512)])
+
+    fill(("TB", 96, 112), 2.0)
+    fill(("TB", 112, 128), 0.5)
+    fill(("TB", 128, 144), 0.0)
+
+    def scan(o, a, b, init, f0, f1):
+        R = [a, b]
+        iv = init
+        if isinstance(init, tuple):
+            R.append(init)
+            iv = P(*init)
+        op("V", lambda q: q.tensor_tensor_scan(P(*o), P(*a), P(*b), iv, f0, f1), R, [o])
+    scan(("TB", 0, 16), ("TB", 112, 128), ("TB", 128, 144), 2.0, A.mult, A.add)
+    for t in range(4):
+        scan(("TB", 32 + 16 * t, 48 + 16 * t), ("TB", 96, 112), ("TB", 128, 144), 0.5, A.mult, A.add)
+    eps = -0.5 + 2.0 ** -13
+    fill(("TB", 17, 28), eps)
+    for j, v in ((16, -0.25), (28, 997 / 4096 + eps), (29, 1994 / 4096 + eps), (30, 5200 / 4096 + eps), (31, 1.0)):
+        fill(("TB", j, j + 1), v)
+    wait("V", {"qV": cnt["V"]})
+    fill(("TB", 12, 14), 2.0 ** -12)
+    fill(("TB", 14, 15), -2.0 ** -12)
+    fill(("TB", 15, 16), 0.0)
+    for t in range(4):
+        b = 32 + 16 * t
+        fill(("TB", b + 12, b + 16), 0.0)
+    wait("V", {"qV": cnt["V"]})
+    for t, fl, wv, cv in ((1, 12, -4096.0, 997.0), (2, 13, -4096.0, 1994.0), (3, 14, 4096.0, -1105.0)):
+        b = 32 + 16 * t
+        fill(("TB", b + fl, b + fl + 1), wv)
+        fill(("TB", b + 15, b + 16), cv)
+
+    ts(("U16", 0, 512), ("U8", 0, 512), -2048.0, A.add, n=8)
+    mm(("VA", 0, 512), ("E8", 0, 128), ("U16", 0, 512), True, False, kn=8)
+    mm(("VA", 0, 512), ("ON", 0, 128), ("K8", 0, 512), False, True, kn=8)
+
+    def cidx(s, v, o, x, y):
+        tt(x, s, v, A.mult)
+        ts(y, x, 5, A.logical_shift_right, 4095, A.bitwise_and)
+        cp(o, y)
+    tt(("CI", 0, 512), ("SRI", 0, 512), ("VA", 0, 512), A.mult)
+    ts(("CJ", 0, 512), ("CI", 0, 512), 5, A.logical_shift_right, 4095, A.bitwise_and)
+    cp(("LW0", 0, 512), ("LMI", 0, 512))
+    cp(("CK", 0, 512), ("CJ", 0, 512))
+
+    def expand(L, a0, a1, i, e="V"):
+        o = T.LX[:, a0 * 16 + i:a1 * 16:16]
+        if e == "V":
+            op("V", lambda q: q.tensor_copy(o, P(L, a0, a1)), [(L, a0, a1)], [("LX", a0 * 16, a1 * 16)])
+        elif e == "G":
+            op("G", lambda q: q.affine_select(o, P(L, a0, a1), [[1, a1 - a0]], A.is_ge, 0.0, 0, 0), [(L, a0, a1)], [("LX", a0 * 16, a1 * 16)])
+        else:
+            op("S", lambda q: q.activation(o, P(L, a0, a1), F.Copy), [(L, a0, a1)], [("LX8", a0 * 16, a1 * 16)])
+    for i in range(16):
+        o = T.LJ[:, i * 128 + i:(i + 1) * 128:16]
+        op("S", lambda q: q.activation(o, T.G8[:], F.Copy), [("G8", 0, 8)], [lj(i)])
+    for k, v in (("NEG", -1.0), ("N8", -8.0), ("P8", 8.0), ("N16", -16.0), ("P16", 16.0), ("M256", -2.0 ** -8), ("P4096", 4096.0)):
+        act(full("I_" + k), full("ID"), F.Copy, scale=v)
+    for i in range(6):
+        expand("LW0", 0, VI, i, "S")
+    for i in range(6, 16):
+        expand("LW0", 0, VI, i)
+    cp(("S0", 0, 512), ("SRI", 0, 512))
+    act(("FL", 0, 512), ("S0", 0, 512), F.Sign, bias=-4095.5)
+    ts(("BJ", 0, 2), ("BI", 0, 2), 15, A.bitwise_and)
+    cp(("BCF", 0, 1), ("BJ", 0, 1))
+    ts(("BCH", 0, 1), ("BCF", 0, 1), -0.5, A.add)
+    ts(("M16", 0, 16), ("JI", 0, 16), ("BCF", 0, 1), A.is_equal)
+    for k in range(6):
+        tt(("TM", 16 * k, 16 * k + 16), ("TB", 16 * k, 16 * k + 16), ("M16", 0, 16), A.mult)
+    for k in range(6):
+        op("V", lambda q: q.tensor_reduce(P("COL", k, k + 1), P("TM", 16 * k, 16 * k + 16), AxisListType.X, A.add),
+           [("TM", 16 * k, 16 * k + 16)], [("COL", k, k + 1)])
+    ts(("KI", 0, 512), ("VA", 0, 512), ("COL", 0, 1), A.mult, ("COL", 1, 2), A.add)
+    for t in range(4):
+        ts(full("WT%d" % t), full("BLK"), ("COL", 2 + t, 3 + t), A.mult)
+    ts(("KJ", 0, 512), ("KI", 0, 512), 1, A.bitwise_and)
+    ts(("W08", 0, 8), ("G8", 0, 8), ("COL", 2, 3), A.mult)
+    ts(("R3", 0, 8), ("R1", 0, 8), 15, A.bitwise_and)
+    cp(("KB0", 0, 512), ("KJ", 0, 512))
+    tt(("R4", 0, 8), ("R3", 0, 8), ("R2", 0, 8), A.add)
+    cp(("RL", 0, 8), ("R4", 0, 8))
+
+    def vcmp(out, lst, a0, n):
+        o, x, l = (out, a0 * 16, (a0 + n) * 16), ("LX", a0 * 16, (a0 + n) * 16), (lst, a0, a0 + n)
+        op("V", lambda q: q.tensor_tensor(P(*o), P(*FW).indirect(P(*l)), P(*x), A.is_gt),
+           [FW, l, x, ("LX8", a0 * 16, (a0 + n) * 16)], [o])
+
+    def vcount(src, a0, n, dst, d0, extra):
+        for i in range(16):
+            mm((dst, d0, d0 + n), lj(i), (src, a0 * 16 + i, (a0 + n) * 16), i == 0, False, step=16)
+        ends(dst, d0, n, extra)
+
+    def ends(dst, d0, n, extra):
+        for k, (w, r) in enumerate(extra):
+            mm((dst, d0, d0 + n), full("I_" + w), r, False, k == len(extra) - 1)
+
+    def sgat(lst, a0, n):
+        sgather(("RS", a0 * 16, (a0 + n) * 16), FW, (lst, a0, a0 + n))
+
+    def sdiff(L, a0, n, h):
+        for k in range(8):
+            d = ("D%d" % h, k * n, k * n + n)
+            mm(d, full("I_NEG"), (L, a0, a0 + n), True, False)
+            mm(d, full("ID"), ("RS", a0 * 16 + 8 * h + k, (a0 + n) * 16), False, True, step=16)
+
+    def ssign(a0, n, h):
+        act(("SG", a0 * 16 + 8 * h * n, a0 * 16 + 8 * h * n + 8 * n), ("D%d" % h, 0, 8 * n), F.Sign, bias=-0.5)
+
+    def scount(a0, n, dst, d0, extra):
+        for i in range(16):
+            mm((dst, d0, d0 + n), lj(i), ("SG", a0 * 16 + i * n, a0 * 16 + (i + 1) * n), i == 0, False)
+        ends(dst, d0, n, extra)
+
+    def schunks(chunks):
+        prev = None
+        for ch in list(chunks) + [None]:
+            if ch is not None:
+                if ch[0]:
+                    if prev is not None and ch[0] not in events:
+                        for y in sfin(prev):
+                            yield y
+                        prev = None
+                    yield ch[0]
+                sgat(ch[1], ch[3], ch[4])
+                yield 16 * ch[4] * GS
+                for h in (0, 1):
+                    if prev is not None and h == 0:
+                        for y in sfin(prev):
+                            yield y
+                    sdiff(ch[2], ch[3], ch[4], h)
+                prev = ch
+            elif prev is not None:
+                for y in sfin(prev):
+                    yield y
+
+    def sfin(ch):
+        for h in (0, 1):
+            ssign(ch[3], ch[4], h)
+            yield 8 * ch[4] * SGN
+        ch[5]()
+        yield ("set", "sg%d" % ch[3])
+
+    events = {}
+
+    def run(streams):
+        events.clear()
+        L = [[s, 0.0, None] for s in streams]
+        while L:
+            ok = [x for x in L if x[2] is None or x[2] in events]
+            assert ok, [x[2] for x in L]
+            x = min(ok, key=lambda x: max(x[1], events.get(x[2], 0.0)))
+            if x[2] is not None:
+                x[1] = max(x[1], events[x[2]])
+                x[2] = None
+            try:
+                y = next(x[0])
+            except StopIteration:
+                L.remove(x)
+                continue
+            if isinstance(y, str):
+                x[2] = y
+            elif isinstance(y, tuple):
+                events[y[1]] = x[1]
+            else:
+                x[1] += y
+
+    def send(dst, src, sem, t):
+        b, lo, hi = src
+        wait("G", deps("G", [src], []))
+        g.remote_dma(P(*dst), P(b, lo, hi), T.sem["r%s%d" % (sem, t)], T.sem.rloc, pid, rid, rmask)
+        remote_total[0] += reng
+
+    def landing(dst, sem, t):
+        acc.setdefault(dst[0], []).append((dst[1], dst[2], "D", ("r%s%d" % (sem, t), reng), True))
+
+    def order(hspec, sregs):
+        for bank, a0, a1, thr in hspec:
+            ts(("HH", a0, a1), (bank, a0, a1), thr, A.is_ge)
+        hh, vb, vc = ("HH", 0, 512), ("VB", 0, 512), ("VC", 0, 512)
+        mm(vb, full("BLK"), hh, True, True)
+        mm(vc, full("BLK"), hh, True, True)
+        mm(("D0", 0, 512), full("I_P4096"), hh, True, True)
+        ts(("OH", 0, 512), vb, 15.0, A.min, ("BCF", 0, 1), A.is_equal)
+        op("S", lambda q: q.activation(T.JUNK[:], P(*vc), F.Sign, bias=T.BCH[:], scale=-1.0, accum_out=T.ACC[:]),
+           [vc, ("BCH", 0, 1)], [("JUNK", 0, 512), ("ACC", 0, 1)])
+        mm(("GDA", 0, 512), full("ID"), ("OH", 0, 512), True, True)
+        scan(("VAL", 0, 512), ("OH", 0, 512), ("OH", 0, 512), ("ACC", 0, 1), A.add, A.add)
+        tt(("PR", 0, 512), ("VAL", 0, 512), ("GDA", 0, 512), A.mult)
+        for j in range(16):
+            mm(("D1", 0, 32), lj(j), ("PR", j, 512), j == 0, j == 15, step=16)
+        for (b, lo, hi), a0 in sregs:
+            tt(("SW", a0, a0 + hi - lo), (b, lo, hi), ("D0", a0, a0 + hi - lo), A.max)
+        ts(("PL", 0, 32), ("D1", 0, 32), 0.5, A.mult, 255.0, A.add)
+        op("V", lambda q: q.tensor_copy(T.OI[:].indirect(T.PL[:]), T.IOT[:]), [("PL", 0, 32), ("IOT", 0, 512)], [("OI", 0, 512)])
+        for j in range(16):
+            mm(("D1", 0, 32), lj(j), ("OI", j, 512), j == 0, j == 15, step=16)
+        ts(("OL", 0, 32), ("D1", 0, 32), 0.0625, A.mult, 256.0, A.add)
+
+    def v_first():
+        yield 3.0
+        for a0 in range(0, VI, 72):
+            vcmp("CM", "CK", a0, 72)
+            yield 16 * 72 * GV
+            vcount("CM", a0, 72, "OVV", a0, [("P8", ("FL", a0, a0 + 72))])
+
+    def s_first():
+        def fin(a0):
+            return lambda: scount(a0, 56, "OVS", a0, [("P16", ("FL", a0, a0 + 56))])
+        for y in schunks([(None, "CK", "LW0", a0, 56, fin(a0)) for a0 in range(VI, 512, 56)]):
+            yield y
+    run([v_first(), s_first()])
+    hspec = [("OVS", VI, 512, -9.0), ("OVV", 0, VI, 3.5)]
+    sregs = [(("S0", 0, 512), 0)]
+
+    for t in range(4):
+        last = t == 3
+        order(hspec, sregs)
+        SO, KB, LW, KL, LL, AR, AW, WRV = ["%s%d" % (k, n) for k, n in (("SO", t), ("KB", t + 1), ("LW", t + 1), ("KL", t), ("LL", t), ("AR", t), ("AW", t), ("WRV", t))]
+        KO, LO = "KB%d" % t, "LW%d" % t
+        VS = V3 if last else VR
+
+        def rob(a0, n):
+            d, d0 = ("GDA", a0) if a0 < 128 else ("VB", a0 - 128)
+            vcount("CMR", a0, n, d, d0, [("N8", ("FL", a0, a0 + n))])
+
+        def finish(h0):
+            d = "GDA" if h0 == 0 else "VB"
+            if h0:
+                k = VS - 128
+                ts(("WB", 128, VS), (d, 0, k), -0.5, A.is_ge, 8192.0, A.mult)
+                ts(("WB", VS, 256), (d, k, 128), -17.0, A.is_ge, 8192.0, A.mult)
+            else:
+                ts(("WB", h0, h0 + 128), (d, 0, 128), -0.5, A.is_ge, 8192.0, A.mult)
+            tt((d, 256, 384), ("SGV", h0, h0 + 128), ("WB", h0, h0 + 128), A.max)
+            tt(("SN", h0, h0 + 128), (SO, h0, h0 + 128), (d, 256, 384), A.min)
+
+        def recv_list(h0):
+            cidx(("SN", h0, h0 + 128), ("VA", h0, h0 + 128), ("CK", h0, h0 + 128), ("CI", h0, h0 + 128), ("CJ", h0, h0 + 128))
+
+        def chk(a0, n):
+            vcount("CM", a0, n, "OVV", a0, [("P8", ("FN", a0, a0 + n))])
+
+        def v_round():
+            vgather((SO, 256, 512), ("SW", 0, 512), ("OL", 16, 32))
+            if not last:
+                send((AR, 0, 128), (SO, 384, 512), "s", t)
+            yield 256 * GV
+            vgather((SO, 0, 256), ("SW", 0, 512), ("OL", 0, 16))
+            yield ("set", "SO")
+            yield 256 * GV
+            yield "v"
+            if not last:
+                cidx((SO, 256, 384), ("VA", 256, 384), ("CK", 256, 384), ("CI", 256, 384), ("CJ", 256, 384))
+                yield 0.35
+                yield ("set", "cD")
+            vgather(("SGV", 0, 128), (SO, 384, 512), ("RL", 0, 8))
+            vgather(("SGV", 128, 256), (SO, 256, 384), ("RL", 0, 8))
+            yield 256 * GV
+            cidx(("SGV", 0, 256), ("VB", 0, 256), ("CR", 0, 256), ("CRI", 0, 256), ("CRJ", 0, 256))
+            yield 0.65
+            yield ("set", "cR")
+            yield "lim"
+            for i in range(16):
+                expand(LW, 0, 128, i)
+            yield 0.85
+            yield "FL"
+            for a0, n in ((0, 64), (64, 64)):
+                vcmp("CMR", "CR", a0, n)
+                yield 16 * n * GV
+                rob(a0, n)
+            yield "LXB"
+            h = (VS - 128) // 2
+            if last:
+                vcmp("CMR", "CR", 128, 2 * h)
+                yield 32 * h * GV
+                rob(128, 2 * h)
+            else:
+                landing((AR, 0, 128), "s", t)
+                landing((KB, 384, 512), "k", t)
+                landing((LW, 384, 512), "l", t)
+                mm(("VC", 0, 128), full("WT%d" % (t + 1)), (KB, 384, 512), True, True)
+                cidx((AR, 0, 128), ("VC", 0, 128), ("CK", 384, 512), ("CI", 384, 512), ("CJ", 384, 512))
+                yield 0.35
+                yield ("set", "cArr")
+                vcmp("CMR", "CR", 128, h)
+                yield 16 * h * GV
+                rob(128, h)
+            finish(0)
+            yield 0.55
+            yield ("set", "wA0")
+            if last:
+                yield ("set", "wA")
+                yield "rA"
+                ts(("OVV", 0, 128), (WRV, 128, 256), -0.5, A.mult, 4096.0, A.add)
+                tt(("DFL", 0, 128), (SO, 384, 512), ("OVV", 0, 128), A.max)
+                send((AR, 0, 128), ("DFL", 0, 128), "s", t)
+                yield "sg%d" % (256 - (256 - VS) // 2)
+                finish(128)
+                yield 0.55
+                yield ("set", "wB")
+                yield "rB"
+                ts(("OVV", 256, 384), (WRV, 0, 128), -0.5, A.mult, 4096.0, A.add)
+                tt(("DF", 0, 128), (SO, 256, 384), ("OVV", 256, 384), A.max)
+                return
+            recv_list(0)
+            yield 0.4
+            yield ("set", "wA")
+            vcmp("CMR", "CR", 128 + h, h)
+            yield 16 * h * GV
+            rob(128 + h, h)
+            for a0, n in ((0, 64), (64, 64)):
+                vcmp("CM", "CK", a0, n)
+                yield 16 * n * GV
+                yield "rA"
+                chk(a0, n)
+            yield "sg%d" % VS
+            finish(128)
+            recv_list(128)
+            yield 0.9
+            yield ("set", "wB")
+            for a0, n in ((128, h), (128 + h, h)):
+                vcmp("CM", "CK", a0, n)
+                yield 16 * n * GV
+                yield "rB"
+                chk(a0, n)
+
+        def rev(h0):
+            o = 128 - h0
+            sgather((WRV, o, o + 128), ("WB", h0, h0 + 128), ("RL", 0, 8))
+            if h0 == 0 and not last:
+                send((AW, 0, 128), (WRV, 128, 256), "w", t)
+            if not last:
+                act(("FN", h0, h0 + 128), ("SN", h0, h0 + 128), F.Sign, bias=-4095.5)
+
+        def s_round():
+            sgather((KB, 0, 384), (KO, 0, 512), ("OL", 0, 24))
+            if not last:
+                mm(("VA", 0, 384), full("WT%d" % (t + 1)), (KB, 0, 384), True, True)
+            mm(("VB", 0, 256), full("WT%d" % t), (KB, 0, 256), True, True)
+            yield 384 * GS
+            yield ("set", "v")
+            sgather((KL, 0, 128), (KO, 0, 512), ("OL", 24, 32))
+            send((KB, 384, 512), (KL, 0, 128), "k", t)
+            yield 128 * GS
+            sgather((LW, 0, 384), (LO, 0, 512), ("OL", 0, 24))
+            yield 384 * GS
+            yield ("set", "lim")
+            sgather((LL, 0, 128), (LO, 0, 512), ("OL", 24, 32))
+            send((LW, 384, 512), (LL, 0, 128), "l", t)
+            yield 128 * GS
+            for i in range(16):
+                expand(LW, 128, VS, i, "G")
+            yield ("set", "LXB")
+            yield "SO"
+            act(("FL", 0, 384), (SO, 0, 384), F.Sign, bias=-4095.5)
+            yield 384 * CYC
+            yield ("set", "FL")
+            if last:
+                act(("YL", 0, 384), (LW, 0, 384), F.Copy)
+                yield 384 * CYC
+                n = (256 - VS) // 2
+
+                def fin(a0):
+                    return lambda: scount(a0, n, "VB", a0 - 128, [("N16", ("FL", a0, a0 + n))])
+                for y in schunks([("cR", "CR", LW, a0, n, fin(a0)) for a0 in (VS, VS + n)]):
+                    yield y
+                return
+            none = lambda: None
+
+            def recv():
+                scount(VS, 256 - VS, "OVS", VS, [("P16", ("FN", VS, 256))])
+
+            def robs():
+                scount(VS, 256 - VS, "VB", VS - 128, [("N16", ("FL", VS, 256))])
+
+            def arr():
+                act(("FL", 384, 512), (AR, 0, 128), F.Sign, bias=-4095.5)
+            for y in schunks([("cD", "CK", LW, 256, 64, none), (None, "CK", LW, 320, 64, none),
+                              ("cR", "CR", LW, VS, 256 - VS, robs), ("cArr", "CK", LW, 384, 64, arr),
+                              (None, "CK", LW, 448, 64, none), ("rB", "CK", LW, VS, 256 - VS, recv)]):
+                yield y
+
+        def s_rev():
+            yield "wA"
+            rev(0)
+            yield 128 * GS
+            yield ("set", "rA")
+            yield "wB"
+            rev(128)
+            yield 128 * GS
+            yield ("set", "rB")
+
+        def t_round():
+            yield "rB"
+            for a0 in (256, 320):
+                yield "sg%d" % a0
+                x = a0 - 256
+                scount(a0, 64, "OVS", a0, [("P16", ("FL", a0, a0 + 64)), ("M256", (WRV, x, x + 64))])
+            yield "rA"
+            landing((AW, 0, 128), "w", t)
+            for a0 in (384, 448):
+                yield "sg%d" % a0
+                x = a0 - 384
+                scount(a0, 64, "OVS", a0, [("P16", ("FL", a0, a0 + 64)), ("M256", (AW, x, x + 64))])
+
+        if last:
+            run([v_round(), s_round(), s_rev()])
+        else:
+            run([v_round(), s_round(), s_rev(), t_round()])
+            hspec = [("OVS", VS, 256, -9.0), ("OVS", 256, 512, -41.0), ("OVV", 0, VS, 3.5)]
+            sregs = [(("SN", 0, 256), 0), ((SO, 256, 384), 256), ((AR, 0, 128), 384)]
+
+    nout = [0]
+
+    def store(dst, src, buf, lo, hi):
+        wait("Y", deps("Y", [(buf, lo, hi)], []))
+        g.sync.dma_start(dst, src).then_inc(T.sem.outs, 16)
+        nout[0] += 16
+    landing(("KB4", 384, 512), "k", 3)
+    landing(("LW4", 384, 512), "l", 3)
+    landing(("AR3", 0, 128), "s", 3)
+    mm(("VC", 0, 512), ("W08", 0, 8), ("KB4", 0, 512), True, True, mn=8)
+    act(("YU", 0, 512), ("VC", 0, 512), F.Copy, n=8)
+    act(("YL", 384, 512), ("LW4", 384, 512), F.Copy)
+    store(T.ylim[:], T.YL[:], "YL", 0, 512)
+    store(T.yu[:], T.YU[:], "YU", 0, 512)
+    store(T.ysr[:, 0:256], T.SN[:], "SN", 0, 256)
+    store(T.ysr[:, 256:384], T.DF[:], "DF", 0, 128)
+    store(T.ysr[:, 384:512], T.AR3[:], "AR3", 0, 128)
+    g.wait_ge(T.sem.rloc, remote_total[0])
+    g.wait_ge(T.sem.outs, nout[0])
+    for e in "VSTG":
+        g.wait_ge(T.sem["q" + e], cnt[e])

@@ -2,19 +2,19 @@ from concourse.mybir import AluOpType as A, AxisListType, ActivationFunctionType
 
 SCRATCH = {
     "FITW": ("sbuf", [128, 4096], "bfloat16"), "SRI": ("sbuf", [128, 512], "int32"), "LMI": ("sbuf", [128, 512], "int32"),
-    "U8": ("sbuf", [8, 512], "int32"), "U16": ("sbuf", [8, 512], "float16"), "K8": ("sbuf", [8, 512], "bfloat16"),
+    "U8": ("sbuf", [8, 512], "int32"), "U16": ("sbuf", [8, 512], "float16"), "K8": ("sbuf", [8, 128], "bfloat16"),
     "E8A": ("sbuf", [8, 128], "bfloat16"), "E8": ("sbuf", [8, 128], "bfloat16"),
     "ON": ("sbuf", [128, 512], "bfloat16"), "ID": ("sbuf", [128, 128], "bfloat16"),
     "BLA": ("sbuf", [128, 128], "bfloat16"), "BLK": ("sbuf", [128, 128], "bfloat16"),
     "G8A": ("sbuf", [128, 8], "bfloat16"), "G8": ("sbuf", [128, 8], "bfloat16"), "LJ": ("sbuf", [128, 2048], "bfloat16"),
     "IOT": ("sbuf", [128, 512], "bfloat16"), "BI": ("sbuf", [128, 2], "int32"), "BJ": ("sbuf", [128, 2], "int32"),
     "BCF": ("sbuf", [128, 1], "float32"), "BCH": ("sbuf", [128, 1], "float32"),
-    "JI": ("sbuf", [128, 16], "float32"), "M16": ("sbuf", [128, 16], "float32"), "TB": ("sbuf", [128, 144], "float32"),
+    "JI": ("sbuf", [128, 96], "float32"), "M16": ("sbuf", [128, 96], "float32"), "TB": ("sbuf", [128, 144], "float32"),
     "TM": ("sbuf", [128, 96], "float32"), "COL": ("sbuf", [128, 8], "float32"), "W08": ("sbuf", [128, 8], "float16"),
     "R1": ("sbuf", [128, 8], "int32"), "R2": ("sbuf", [128, 8], "int32"), "R3": ("sbuf", [128, 8], "int32"),
     "R4": ("sbuf", [128, 8], "int32"), "RL": ("sbuf", [128, 8], "uint16"),
     "KI": ("sbuf", [128, 512], "int32"), "KJ": ("sbuf", [128, 512], "int32"),
-    "S0": ("sbuf", [128, 512], "float32"), "SW": ("sbuf", [128, 512], "float32"), "SN": ("sbuf", [128, 256], "float32"),
+    "SW": ("sbuf", [128, 512], "float32"), "SN": ("sbuf", [128, 256], "float32"),
     "SGV": ("sbuf", [128, 256], "float32"), "FN": ("sbuf", [128, 256], "bfloat16"), "WB": ("sbuf", [128, 256], "bfloat16"),
     "FL": ("sbuf", [128, 512], "bfloat16"), "CI": ("sbuf", [128, 512], "int32"), "CJ": ("sbuf", [128, 512], "int32"),
     "CRI": ("sbuf", [128, 256], "int32"), "CRJ": ("sbuf", [128, 256], "int32"),
@@ -24,10 +24,10 @@ SCRATCH = {
     "HH": ("sbuf", [128, 512], "bfloat16"), "OH": ("sbuf", [128, 512], "bfloat16"), "JUNK": ("sbuf", [128, 512], "bfloat16"),
     "ACC": ("sbuf", [128, 1], "float32"), "VAL": ("sbuf", [128, 512], "bfloat16"), "PR": ("sbuf", [128, 512], "bfloat16"),
     "PL": ("sbuf", [128, 32], "uint16"), "OI": ("sbuf", [128, 512], "bfloat16"), "OL": ("sbuf", [128, 32], "uint16"),
-    "DFL": ("sbuf", [128, 128], "float32"), "DF": ("sbuf", [128, 128], "float32"),
+    "DM": ("sbuf", [128, 256], "float32"), "DFL": ("sbuf", [128, 128], "float32"), "DF": ("sbuf", [128, 128], "float32"),
     "YL": ("sbuf", [128, 512], "float32"), "YU": ("sbuf", [8, 512], "float32"),
 }
-for _w in ("N8", "P8", "N16", "P16", "M256", "NEG", "P4096"):
+for _w in ("N8", "P8", "N16", "P16", "NEG", "P4096"):
     SCRATCH["I_" + _w] = ("sbuf", [128, 128], "bfloat16")
 for _t in range(4):
     SCRATCH["WT%d" % _t] = ("sbuf", [128, 128], "float16")
@@ -48,8 +48,9 @@ SEMAPHORES += ["r%s%d" % (_k, _t) for _k in "sklw" for _t in range(4)]
 
 CYC = 0.00083
 GV, GS, SGN = 1.5 * CYC, 1.5 * CYC, 1.0 * CYC
-VI = 288
-VR, V3 = 220, 160
+VI, NV, NS = 320, 80, 64
+VR = 180
+V3 = 72
 
 
 def rank_program(g, core, T, topo):
@@ -190,20 +191,18 @@ def rank_program(g, core, T, topo):
     def fill(o, v, n=128):
         op("V", lambda q: q.memset(P(*o, n), v), [], [o])
     fill(("ON", 0, 512), 1.0)
-    fill(("K8", 0, 512), 256.0, 8)
-    fill(("LJ", 0, 2048), 0.0)
+    fill(("K8", 0, 128), 256.0, 8)
+    op("G", lambda q: q.iota(T.BI[:, 0:2], [[0, 2]], 0, 1), [], [("BI", 0, 2)])
+    op("G", lambda q: q.iota(T.JI[:], [[0, 6], [1, 16]], 0, 0, allow_small_or_imprecise_dtypes=True), [], [("JI", 0, 96)])
+    op("G", lambda q: q.iota(T.R1[:], [[0, 8]], 127, -1), [], [("R1", 0, 8)])
+    op("G", lambda q: q.iota(T.R2[:], [[-16, 8]], 112, 0), [], [("R2", 0, 8)])
     sel(("E8A", 0, 128), ("ON", 0, 128), [[1, 128]], A.is_ge, 0, -16, 8)
     sel(("E8", 0, 128), ("E8A", 0, 128), [[-1, 128]], A.is_ge, 15, 16, 8)
-    op("G", lambda q: q.iota(T.BI[:, 0:2], [[0, 2]], 0, 1), [], [("BI", 0, 2)])
-    op("G", lambda q: q.iota(T.JI[:], [[1, 16]], 0, 0, allow_small_or_imprecise_dtypes=True), [], [("JI", 0, 16)])
     sel(("G8A", 0, 8), ("ON", 0, 8), [[-16, 8]], A.is_ge, 0, 1)
     sel(("G8", 0, 8), ("G8A", 0, 8), [[16, 8]], A.is_ge, 15, -1)
     sel(full("ID"), ("ON", 0, 128), [[-1, 128]], A.is_equal, 0, 1)
     sel(full("BLA"), ("ON", 0, 128), [[-16, 8], [0, 16]], A.is_ge, 0, 1)
     sel(full("BLK"), full("BLA"), [[16, 8], [0, 16]], A.is_ge, 15, -1)
-    op("G", lambda q: q.iota(T.R1[:], [[0, 8]], 127, -1), [], [("R1", 0, 8)])
-    op("G", lambda q: q.iota(T.R2[:], [[-16, 8]], 112, 0), [], [("R2", 0, 8)])
-    op("G", lambda q: q.iota(T.IOT[:], [[1, 512]], -256, 0, allow_small_or_imprecise_dtypes=True), [], [("IOT", 0, 512)])
 
     fill(("TB", 96, 112), 2.0)
     fill(("TB", 112, 128), 0.5)
@@ -219,78 +218,83 @@ def rank_program(g, core, T, topo):
     scan(("TB", 0, 16), ("TB", 112, 128), ("TB", 128, 144), 2.0, A.mult, A.add)
     for t in range(4):
         scan(("TB", 32 + 16 * t, 48 + 16 * t), ("TB", 96, 112), ("TB", 128, 144), 0.5, A.mult, A.add)
-    eps = -0.5 + 2.0 ** -13
-    fill(("TB", 17, 28), eps)
-    for j, v in ((16, -0.25), (28, 997 / 4096 + eps), (29, 1994 / 4096 + eps), (30, 5200 / 4096 + eps), (31, 1.0)):
-        fill(("TB", j, j + 1), v)
-    wait("V", {"qV": cnt["V"]})
-    fill(("TB", 12, 14), 2.0 ** -12)
-    fill(("TB", 14, 15), -2.0 ** -12)
-    fill(("TB", 15, 16), 0.0)
-    for t in range(4):
-        b = 32 + 16 * t
-        fill(("TB", b + 12, b + 16), 0.0)
-    wait("V", {"qV": cnt["V"]})
-    for t, fl, wv, cv in ((1, 12, -4096.0, 997.0), (2, 13, -4096.0, 1994.0), (3, 14, 4096.0, -1105.0)):
-        b = 32 + 16 * t
-        fill(("TB", b + fl, b + fl + 1), wv)
-        fill(("TB", b + 15, b + 16), cv)
+    ts(("BJ", 0, 2), ("BI", 0, 2), 15, A.bitwise_and)
+    cp(("BCF", 0, 1), ("BJ", 0, 1))
+    ts(("BCH", 0, 1), ("BCF", 0, 1), -0.5, A.add)
+    ts(("M16", 0, 96), ("JI", 0, 96), ("BCF", 0, 1), A.is_equal)
+    ts(("R3", 0, 8), ("R1", 0, 8), 15, A.bitwise_and)
+    tt(("R4", 0, 8), ("R3", 0, 8), ("R2", 0, 8), A.add)
+    cp(("RL", 0, 8), ("R4", 0, 8))
 
     ts(("U16", 0, 512), ("U8", 0, 512), -2048.0, A.add, n=8)
-    mm(("VA", 0, 512), ("E8", 0, 128), ("U16", 0, 512), True, False, kn=8)
-    mm(("VA", 0, 512), ("ON", 0, 128), ("K8", 0, 512), False, True, kn=8)
-
-    def cidx(s, v, o, x, y):
-        tt(x, s, v, A.mult)
-        ts(y, x, 5, A.logical_shift_right, 4095, A.bitwise_and)
-        cp(o, y)
-    tt(("CI", 0, 512), ("SRI", 0, 512), ("VA", 0, 512), A.mult)
-    ts(("CJ", 0, 512), ("CI", 0, 512), 5, A.logical_shift_right, 4095, A.bitwise_and)
     cp(("LW0", 0, 512), ("LMI", 0, 512))
-    cp(("CK", 0, 512), ("CJ", 0, 512))
+    mm(("VA", 0, 512), ("E8", 0, 128), ("U16", 0, 512), True, False, kn=8)
+    mm(("VA", 0, 512), ("K8", 0, 128), ("ON", 0, 512), False, True, kn=8)
+
+    def chain(s, v, o, x, y):
+        return [lambda: tt(x, s, v, A.mult), lambda: ts(y, x, 5, A.logical_shift_right, 4095, A.bitwise_and), lambda: cp(o, y)]
+
+    def cidx(*a):
+        for f in chain(*a):
+            f()
+    cidx(("SRI", 0, 512), ("VA", 0, 512), ("CK", 0, 512), ("CI", 0, 512), ("CJ", 0, 512))
+    ts(("FL", 0, 512), ("SRI", 0, 512), 4096.0, A.is_ge)
 
     def expand(L, a0, a1, i, e="V"):
         o = T.LX[:, a0 * 16 + i:a1 * 16:16]
         if e == "V":
             op("V", lambda q: q.tensor_copy(o, P(L, a0, a1)), [(L, a0, a1)], [("LX", a0 * 16, a1 * 16)])
         elif e == "G":
-            op("G", lambda q: q.affine_select(o, P(L, a0, a1), [[1, a1 - a0]], A.is_ge, 0.0, 0, 0), [(L, a0, a1)], [("LX", a0 * 16, a1 * 16)])
+            op("G", lambda q: q.affine_select(o, P(L, a0, a1), [[1, a1 - a0]], A.is_ge, 0.0, 0, 0), [(L, a0, a1)], [("LX9", a0 * 16, a1 * 16)])
         else:
             op("S", lambda q: q.activation(o, P(L, a0, a1), F.Copy), [(L, a0, a1)], [("LX8", a0 * 16, a1 * 16)])
+    for i in range(4):
+        act(("LJ", 512 * i, 512 * i + 512), ("ON", 0, 512), F.Copy, scale=0.0)
+    wait("S", {"qS": cnt["S"]})
     for i in range(16):
         o = T.LJ[:, i * 128 + i:(i + 1) * 128:16]
         op("S", lambda q: q.activation(o, T.G8[:], F.Copy), [("G8", 0, 8)], [lj(i)])
-    for k, v in (("NEG", -1.0), ("N8", -8.0), ("P8", 8.0), ("N16", -16.0), ("P16", 16.0), ("M256", -2.0 ** -8), ("P4096", 4096.0)):
+    for k, v in (("NEG", -1.0), ("N8", -8.0), ("P8", 8.0), ("N16", -16.0), ("P16", 16.0), ("P4096", 4096.0)):
         act(full("I_" + k), full("ID"), F.Copy, scale=v)
-    for i in range(6):
+    for i in range(5):
         expand("LW0", 0, VI, i, "S")
-    for i in range(6, 16):
+    for i in range(5, 10):
+        expand("LW0", 0, VI, i, "G")
+    for i in range(10, 16):
         expand("LW0", 0, VI, i)
-    cp(("S0", 0, 512), ("SRI", 0, 512))
-    act(("FL", 0, 512), ("S0", 0, 512), F.Sign, bias=-4095.5)
-    ts(("BJ", 0, 2), ("BI", 0, 2), 15, A.bitwise_and)
-    cp(("BCF", 0, 1), ("BJ", 0, 1))
-    ts(("BCH", 0, 1), ("BCF", 0, 1), -0.5, A.add)
-    ts(("M16", 0, 16), ("JI", 0, 16), ("BCF", 0, 1), A.is_equal)
-    for k in range(6):
-        tt(("TM", 16 * k, 16 * k + 16), ("TB", 16 * k, 16 * k + 16), ("M16", 0, 16), A.mult)
-    for k in range(6):
-        op("V", lambda q: q.tensor_reduce(P("COL", k, k + 1), P("TM", 16 * k, 16 * k + 16), AxisListType.X, A.add),
-           [("TM", 16 * k, 16 * k + 16)], [("COL", k, k + 1)])
-    ts(("KI", 0, 512), ("VA", 0, 512), ("COL", 0, 1), A.mult, ("COL", 1, 2), A.add)
-    for t in range(4):
-        ts(full("WT%d" % t), full("BLK"), ("COL", 2 + t, 3 + t), A.mult)
-    ts(("KJ", 0, 512), ("KI", 0, 512), 1, A.bitwise_and)
-    ts(("W08", 0, 8), ("G8", 0, 8), ("COL", 2, 3), A.mult)
-    ts(("R3", 0, 8), ("R1", 0, 8), 15, A.bitwise_and)
-    cp(("KB0", 0, 512), ("KJ", 0, 512))
-    tt(("R4", 0, 8), ("R3", 0, 8), ("R2", 0, 8), A.add)
-    cp(("RL", 0, 8), ("R4", 0, 8))
+
+    def gfill(lo, hi, v):
+        op("G", lambda q: q.affine_select(P("TB", lo, hi), P("JI", 0, hi - lo), [[0, hi - lo]], A.is_gt, v, 0, 0), [("JI", 0, 16)], [("TB", lo, hi)])
+    eps = -0.5 + 2.0 ** -13
+    gfill(17, 28, eps)
+    for j, v in ((16, -0.25), (28, 997 / 4096 + eps), (29, 1994 / 4096 + eps), (30, 5200 / 4096 + eps), (31, 1.0)):
+        gfill(j, j + 1, v)
+    gfill(12, 14, 2.0 ** -12)
+    gfill(14, 15, -2.0 ** -12)
+    gfill(15, 16, 0.0)
+    gfill(44, 48, 0.0)
+    for t, w in ((1, (-4096.0, 0.0, 0.0, 997.0)), (2, (0.0, -4096.0, 0.0, 1994.0)), (3, (0.0, 0.0, 4096.0, -1105.0))):
+        for j in range(4):
+            gfill(44 + 16 * t + j, 45 + 16 * t + j, w[j])
+    op("G", lambda q: q.iota(T.IOT[:], [[1, 512]], -256, 0, allow_small_or_imprecise_dtypes=True), [], [("IOT", 0, 512)])
+
+    def columns():
+        tt(("TM", 0, 96), ("TB", 0, 96), ("M16", 0, 96), A.mult)
+        for k in range(6):
+            op("V", lambda q: q.tensor_reduce(P("COL", k, k + 1), P("TM", 16 * k, 16 * k + 16), AxisListType.X, A.add),
+               [("TM", 16 * k, 16 * k + 16)], [("COL", k, k + 1)])
+        weights(0)
+
+    def weights(t0):
+        for t in (t0, t0 + 1):
+            ts(full("WT%d" % t), full("BLK"), ("COL", 2 + t, 3 + t), A.mult)
+        if t0:
+            ts(("W08", 0, 8), ("G8", 0, 8), ("COL", 2, 3), A.mult)
 
     def vcmp(out, lst, a0, n):
         o, x, l = (out, a0 * 16, (a0 + n) * 16), ("LX", a0 * 16, (a0 + n) * 16), (lst, a0, a0 + n)
         op("V", lambda q: q.tensor_tensor(P(*o), P(*FW).indirect(P(*l)), P(*x), A.is_gt),
-           [FW, l, x, ("LX8", a0 * 16, (a0 + n) * 16)], [o])
+           [FW, l, x, ("LX8", a0 * 16, (a0 + n) * 16), ("LX9", a0 * 16, (a0 + n) * 16)], [o])
 
     def vcount(src, a0, n, dst, d0, extra):
         for i in range(16):
@@ -331,10 +335,13 @@ def rank_program(g, core, T, topo):
                 sgat(ch[1], ch[3], ch[4])
                 yield 16 * ch[4] * GS
                 for h in (0, 1):
-                    if prev is not None and h == 0:
-                        for y in sfin(prev):
-                            yield y
+                    if prev is not None:
+                        ssign(prev[3], prev[4], h)
+                        yield 8 * prev[4] * SGN
                     sdiff(ch[2], ch[3], ch[4], h)
+                if prev is not None:
+                    prev[5]()
+                    yield ("set", "sg%d" % prev[3])
                 prev = ch
             elif prev is not None:
                 for y in sfin(prev):
@@ -380,17 +387,25 @@ def rank_program(g, core, T, topo):
     def landing(dst, sem, t):
         acc.setdefault(dst[0], []).append((dst[1], dst[2], "D", ("r%s%d" % (sem, t), reng), True))
 
-    def order(hspec, sregs):
+    def order(hspec, sregs, t):
+        first = t == 0
         for bank, a0, a1, thr in hspec:
-            ts(("HH", a0, a1), (bank, a0, a1), thr, A.is_ge)
+            if isinstance(thr, tuple):
+                tt(("HH", a0, a1), (bank, a0, a1), thr, A.is_ge)
+            else:
+                ts(("HH", a0, a1), (bank, a0, a1), thr, A.is_ge)
+            mm(("VC", a0, a1), full("BLK"), ("HH", a0, a1), True, True)
+            mm(("VB", a0, a1), full("BLK"), ("HH", a0, a1), True, True)
         hh, vb, vc = ("HH", 0, 512), ("VB", 0, 512), ("VC", 0, 512)
-        mm(vb, full("BLK"), hh, True, True)
-        mm(vc, full("BLK"), hh, True, True)
         mm(("D0", 0, 512), full("I_P4096"), hh, True, True)
+        if first:
+            ts(("KI", 0, 512), ("VA", 0, 512), ("COL", 0, 1), A.mult, ("COL", 1, 2), A.add)
         ts(("OH", 0, 512), vb, 15.0, A.min, ("BCF", 0, 1), A.is_equal)
         op("S", lambda q: q.activation(T.JUNK[:], P(*vc), F.Sign, bias=T.BCH[:], scale=-1.0, accum_out=T.ACC[:]),
            [vc, ("BCH", 0, 1)], [("JUNK", 0, 512), ("ACC", 0, 1)])
         mm(("GDA", 0, 512), full("ID"), ("OH", 0, 512), True, True)
+        if first:
+            ts(("KJ", 0, 512), ("KI", 0, 512), 1, A.bitwise_and)
         scan(("VAL", 0, 512), ("OH", 0, 512), ("OH", 0, 512), ("ACC", 0, 1), A.add, A.add)
         tt(("PR", 0, 512), ("VAL", 0, 512), ("GDA", 0, 512), A.mult)
         for j in range(16):
@@ -399,45 +414,56 @@ def rank_program(g, core, T, topo):
             tt(("SW", a0, a0 + hi - lo), (b, lo, hi), ("D0", a0, a0 + hi - lo), A.max)
         ts(("PL", 0, 32), ("D1", 0, 32), 0.5, A.mult, 255.0, A.add)
         op("V", lambda q: q.tensor_copy(T.OI[:].indirect(T.PL[:]), T.IOT[:]), [("PL", 0, 32), ("IOT", 0, 512)], [("OI", 0, 512)])
+        if first:
+            cp(("KB0", 0, 512), ("KJ", 0, 512))
+        if t == 1:
+            weights(2)
         for j in range(16):
             mm(("D1", 0, 32), lj(j), ("OI", j, 512), j == 0, j == 15, step=16)
         ts(("OL", 0, 32), ("D1", 0, 32), 0.0625, A.mult, 256.0, A.add)
 
     def v_first():
-        yield 3.0
-        for a0 in range(0, VI, 72):
-            vcmp("CM", "CK", a0, 72)
-            yield 16 * 72 * GV
-            vcount("CM", a0, 72, "OVV", a0, [("P8", ("FL", a0, a0 + 72))])
+        for a0 in range(0, VI, NV):
+            vcmp("CM", "CK", a0, NV)
+            if a0 + NV == VI:
+                columns()
+            yield 16 * NV * GV
+            vcount("CM", a0, NV, "OVV", a0, [("P16", ("FL", a0, a0 + NV))])
 
     def s_first():
         def fin(a0):
-            return lambda: scount(a0, 56, "OVS", a0, [("P16", ("FL", a0, a0 + 56))])
-        for y in schunks([(None, "CK", "LW0", a0, 56, fin(a0)) for a0 in range(VI, 512, 56)]):
+            return lambda: scount(a0, NS, "OVS", a0, [("P16", ("FL", a0, a0 + NS))] * 2)
+        for y in schunks([(None, "CK", "LW0", a0, NS, fin(a0)) for a0 in range(VI, 512, NS)]):
             yield y
     run([v_first(), s_first()])
-    hspec = [("OVS", VI, 512, -9.0), ("OVV", 0, VI, 3.5)]
-    sregs = [(("S0", 0, 512), 0)]
+    hspec = [("OVV", 0, VI, 11.5), ("OVS", VI, 512, 7.0)]
+    sregs = [(("SRI", 0, 512), 0)]
 
     for t in range(4):
         last = t == 3
-        order(hspec, sregs)
+        order(hspec, sregs, t)
         SO, KB, LW, KL, LL, AR, AW, WRV = ["%s%d" % (k, n) for k, n in (("SO", t), ("KB", t + 1), ("LW", t + 1), ("KL", t), ("LL", t), ("AR", t), ("AW", t), ("WRV", t))]
         KO, LO = "KB%d" % t, "LW%d" % t
-        VS = V3 if last else VR
+        VS = 128 + V3 if last else VR
+        VA3 = V3 if last else 128
+        NR = (256 - VS) // 2
 
         def rob(a0, n):
             d, d0 = ("GDA", a0) if a0 < 128 else ("VB", a0 - 128)
             vcount("CMR", a0, n, d, d0, [("N8", ("FL", a0, a0 + n))])
 
-        def finish(h0):
+        def finish(h0, final=None, so=None):
             d = "GDA" if h0 == 0 else "VB"
-            if h0:
-                k = VS - 128
-                ts(("WB", 128, VS), (d, 0, k), -0.5, A.is_ge, 8192.0, A.mult)
-                ts(("WB", VS, 256), (d, k, 128), -17.0, A.is_ge, 8192.0, A.mult)
-            else:
-                ts(("WB", h0, h0 + 128), (d, 0, 128), -0.5, A.is_ge, 8192.0, A.mult)
+            k = VS - 128 if h0 else VA3
+            ts(("WB", h0, h0 + k), (d, 0, k), -0.5, A.is_ge, 8192.0, A.mult)
+            if k < 128:
+                ts(("WB", h0 + k, h0 + 128), (d, k, 128), -17.0, A.is_ge, 8192.0, A.mult)
+            if final:
+                op("V", lambda q: q.tensor_scalar(T.DM[:, h0:h0 + 128], T.WB[:, h0:h0 + 128].indirect(T.RL[:]), -0.5, 4096.0, A.mult, A.add),
+                   [("WB", h0, h0 + 128), ("RL", 0, 8)], [("DM", h0, h0 + 128)])
+                tt((final, 0, 128), so, ("DM", h0, h0 + 128), A.max)
+                if h0 == 0:
+                    send((AR, 0, 128), (final, 0, 128), "s", t)
             tt((d, 256, 384), ("SGV", h0, h0 + 128), ("WB", h0, h0 + 128), A.max)
             tt(("SN", h0, h0 + 128), (SO, h0, h0 + 128), (d, 256, 384), A.min)
 
@@ -456,88 +482,82 @@ def rank_program(g, core, T, topo):
             yield ("set", "SO")
             yield 256 * GV
             yield "v"
-            if not last:
-                cidx((SO, 256, 384), ("VA", 256, 384), ("CK", 256, 384), ("CI", 256, 384), ("CJ", 256, 384))
-                yield 0.35
+            if last:
+                vgather(("SGV", 0, 128), (SO, 384, 512), ("RL", 0, 8))
+                cidx(("SGV", 0, 128), ("VB", 0, 128), ("CR", 0, 128), ("CRI", 0, 128), ("CRJ", 0, 128))
+                yield 0.55
+            else:
+                cD = chain((SO, 256, 384), ("VA", 256, 384), ("CK", 256, 384), ("CI", 256, 384), ("CJ", 256, 384))
+                cD[0]()
+                vgather(("SGV", 0, 128), (SO, 384, 512), ("RL", 0, 8))
+                cD[1]()
+                vgather(("SGV", 128, 256), (SO, 256, 384), ("RL", 0, 8))
+                cD[2]()
+                yield 256 * GV + 0.35
                 yield ("set", "cD")
-            vgather(("SGV", 0, 128), (SO, 384, 512), ("RL", 0, 8))
-            vgather(("SGV", 128, 256), (SO, 256, 384), ("RL", 0, 8))
-            yield 256 * GV
-            cidx(("SGV", 0, 256), ("VB", 0, 256), ("CR", 0, 256), ("CRI", 0, 256), ("CRJ", 0, 256))
-            yield 0.65
+                cidx(("SGV", 0, 256), ("VB", 0, 256), ("CR", 0, 256), ("CRI", 0, 256), ("CRJ", 0, 256))
+                yield 0.65
             yield ("set", "cR")
             yield "lim"
             for i in range(16):
-                expand(LW, 0, 128, i)
+                expand(LW, 0, VA3, i)
             yield 0.85
             yield "FL"
-            for a0, n in ((0, 64), (64, 64)):
+            for a0, n in ((0, V3),) if last else ((0, 64), (64, 64)):
                 vcmp("CMR", "CR", a0, n)
-                yield 16 * n * GV
+                yield 16 * n * GV * (0.3 if a0 == 64 else 1)
+                if a0 == 64:
+                    landing((AR, 0, 128), "s", t)
+                    landing((KB, 384, 512), "k", t)
+                    landing((LW, 384, 512), "l", t)
+                    mm(("VC", 0, 128), full("WT%d" % (t + 1)), (KB, 384, 512), True, True)
+                    yield 16 * n * GV * 0.7
                 rob(a0, n)
-            yield "LXB"
-            h = (VS - 128) // 2
             if last:
-                vcmp("CMR", "CR", 128, 2 * h)
-                yield 32 * h * GV
-                rob(128, 2 * h)
-            else:
-                landing((AR, 0, 128), "s", t)
-                landing((KB, 384, 512), "k", t)
-                landing((LW, 384, 512), "l", t)
-                mm(("VC", 0, 128), full("WT%d" % (t + 1)), (KB, 384, 512), True, True)
-                cidx((AR, 0, 128), ("VC", 0, 128), ("CK", 384, 512), ("CI", 384, 512), ("CJ", 384, 512))
-                yield 0.35
-                yield ("set", "cArr")
-                vcmp("CMR", "CR", 128, h)
-                yield 16 * h * GV
-                rob(128, h)
+                vgather(("SGV", 128, 256), (SO, 256, 384), ("RL", 0, 8))
+                cidx(("SGV", 128, 256), ("VB", 128, 256), ("CR", 128, 256), ("CRI", 128, 256), ("CRJ", 128, 256))
+                yield ("set", "cRB")
+                yield "sg%d" % V3
+                finish(0, "DFL", (SO, 384, 512))
+                yield 0.9
+                yield "LXB"
+                vcmp("CMR", "CR", 128, V3)
+                yield 16 * V3 * GV
+                rob(128, V3)
+                yield "sg%d" % VS
+                finish(128, "DF", (SO, 256, 384))
+                return
+            cidx((AR, 0, 128), ("VC", 0, 128), ("CK", 384, 512), ("CI", 384, 512), ("CJ", 384, 512))
+            yield 0.35
+            yield ("set", "cArr")
+            yield "LXB"
+            vcmp("CMR", "CR", 128, VS - 128)
+            yield 16 * (VS - 128) * GV
+            rob(128, VS - 128)
             finish(0)
             yield 0.55
-            yield ("set", "wA0")
-            if last:
-                yield ("set", "wA")
-                yield "rA"
-                ts(("OVV", 0, 128), (WRV, 128, 256), -0.5, A.mult, 4096.0, A.add)
-                tt(("DFL", 0, 128), (SO, 384, 512), ("OVV", 0, 128), A.max)
-                send((AR, 0, 128), ("DFL", 0, 128), "s", t)
-                yield "sg%d" % (256 - (256 - VS) // 2)
-                finish(128)
-                yield 0.55
-                yield ("set", "wB")
-                yield "rB"
-                ts(("OVV", 256, 384), (WRV, 0, 128), -0.5, A.mult, 4096.0, A.add)
-                tt(("DF", 0, 128), (SO, 256, 384), ("OVV", 256, 384), A.max)
-                return
             recv_list(0)
             yield 0.4
             yield ("set", "wA")
-            vcmp("CMR", "CR", 128 + h, h)
-            yield 16 * h * GV
-            rob(128 + h, h)
-            for a0, n in ((0, 64), (64, 64)):
-                vcmp("CM", "CK", a0, n)
-                yield 16 * n * GV
-                yield "rA"
-                chk(a0, n)
-            yield "sg%d" % VS
-            finish(128)
-            recv_list(128)
-            yield 0.9
-            yield ("set", "wB")
-            for a0, n in ((128, h), (128 + h, h)):
-                vcmp("CM", "CK", a0, n)
-                yield 16 * n * GV
-                yield "rB"
-                chk(a0, n)
+            for a0 in (0, 64, 128, 192):
+                if a0 == 128:
+                    yield "sg%d" % (256 - NR)
+                    finish(128)
+                    recv_list(128)
+                    yield 0.9
+                    yield ("set", "wB")
+                vcmp("CM", "CK", a0, 64)
+                yield 1024 * GV
+                yield "rB" if a0 >= 128 else "rA"
+                chk(a0, 64)
 
         def rev(h0):
             o = 128 - h0
-            sgather((WRV, o, o + 128), ("WB", h0, h0 + 128), ("RL", 0, 8))
-            if h0 == 0 and not last:
+            op("S", lambda q: q.activation(P(WRV, o, o + 128), T.WB[:, h0:h0 + 128].indirect(T.RL[:]), F.Identity, bias=-41.0, scale=2.0 ** -8),
+               [("WB", h0, h0 + 128), ("RL", 0, 8)], [(WRV, o, o + 128)])
+            if h0 == 0:
                 send((AW, 0, 128), (WRV, 128, 256), "w", t)
-            if not last:
-                act(("FN", h0, h0 + 128), ("SN", h0, h0 + 128), F.Sign, bias=-4095.5)
+            act(("FN", h0, h0 + 128), ("SN", h0, h0 + 128), F.Sign, bias=-4095.5)
 
         def s_round():
             sgather((KB, 0, 384), (KO, 0, 512), ("OL", 0, 24))
@@ -558,33 +578,47 @@ def rank_program(g, core, T, topo):
             for i in range(16):
                 expand(LW, 128, VS, i, "G")
             yield ("set", "LXB")
+            if not last:
+                for i in range(16):
+                    expand(LW, VS, 256, i, "G")
             yield "SO"
             act(("FL", 0, 384), (SO, 0, 384), F.Sign, bias=-4095.5)
             yield 384 * CYC
             yield ("set", "FL")
             if last:
-                act(("YL", 0, 384), (LW, 0, 384), F.Copy)
-                yield 384 * CYC
-                n = (256 - VS) // 2
-
-                def fin(a0):
-                    return lambda: scount(a0, n, "VB", a0 - 128, [("N16", ("FL", a0, a0 + n))])
-                for y in schunks([("cR", "CR", LW, a0, n, fin(a0)) for a0 in (VS, VS + n)]):
-                    yield y
+                n = 128 - V3
+                yield "cR"
+                for a0, d in ((V3, "GDA"), (VS, "VB")):
+                    if d == "VB":
+                        yield "cRB"
+                    sgat("CR", a0, n)
+                    yield 16 * n * GS
+                    sdiff(LW, a0, n, 0)
+                    sdiff(LW, a0, n, 1)
+                    if d == "GDA":
+                        act(("YL", 0, 384), (LW, 0, 384), F.Copy)
+                        yield 384 * CYC
+                    for y in sfin((None, None, None, a0, n, lambda: scount(a0, n, d, V3, [("N16", ("FL", a0, a0 + n))]))):
+                        yield y
+                landing(("KB4", 384, 512), "k", 3)
+                landing(("LW4", 384, 512), "l", 3)
+                mm(("VC", 0, 512), ("W08", 0, 8), ("KB4", 0, 512), True, True, mn=8)
+                act(("YU", 0, 512), ("VC", 0, 512), F.Copy, n=8)
+                act(("YL", 384, 512), ("LW4", 384, 512), F.Copy)
                 return
-            none = lambda: None
 
-            def recv():
-                scount(VS, 256 - VS, "OVS", VS, [("P16", ("FN", VS, 256))])
+            def don(a0):
+                return lambda: scount(a0, 64, "OVS", a0, [("P16", ("FL", a0, a0 + 64))])
 
-            def robs():
-                scount(VS, 256 - VS, "VB", VS - 128, [("N16", ("FL", VS, 256))])
+            def robs(a0):
+                return lambda: scount(a0, NR, "VB", a0 - 128, [("N16", ("FL", a0, a0 + NR))])
 
             def arr():
                 act(("FL", 384, 512), (AR, 0, 128), F.Sign, bias=-4095.5)
-            for y in schunks([("cD", "CK", LW, 256, 64, none), (None, "CK", LW, 320, 64, none),
-                              ("cR", "CR", LW, VS, 256 - VS, robs), ("cArr", "CK", LW, 384, 64, arr),
-                              (None, "CK", LW, 448, 64, none), ("rB", "CK", LW, VS, 256 - VS, recv)]):
+                don(384)()
+            for y in schunks([("cD", "CK", LW, 256, 64, don(256)),
+                              ("cR", "CR", LW, VS, NR, robs(VS)), ("cR", "CR", LW, VS + NR, NR, robs(VS + NR)),
+                              (None, "CK", LW, 320, 64, don(320)), ("cArr", "CK", LW, 384, 64, arr), (None, "CK", LW, 448, 64, don(448))]):
                 yield y
 
         def s_rev():
@@ -597,24 +631,10 @@ def rank_program(g, core, T, topo):
             yield 128 * GS
             yield ("set", "rB")
 
-        def t_round():
-            yield "rB"
-            for a0 in (256, 320):
-                yield "sg%d" % a0
-                x = a0 - 256
-                scount(a0, 64, "OVS", a0, [("P16", ("FL", a0, a0 + 64)), ("M256", (WRV, x, x + 64))])
-            yield "rA"
+        run([v_round(), s_round()] + ([] if last else [s_rev()]))
+        if not last:
             landing((AW, 0, 128), "w", t)
-            for a0 in (384, 448):
-                yield "sg%d" % a0
-                x = a0 - 384
-                scount(a0, 64, "OVS", a0, [("P16", ("FL", a0, a0 + 64)), ("M256", (AW, x, x + 64))])
-
-        if last:
-            run([v_round(), s_round(), s_rev()])
-        else:
-            run([v_round(), s_round(), s_rev(), t_round()])
-            hspec = [("OVS", VS, 256, -9.0), ("OVS", 256, 512, -41.0), ("OVV", 0, VS, 3.5)]
+            hspec = [("OVS", 256, 384, (WRV, 0, 128)), ("OVS", 384, 512, (AW, 0, 128)), ("OVV", 0, 256, 3.5)]
             sregs = [(("SN", 0, 256), 0), ((SO, 256, 384), 256), ((AR, 0, 128), 384)]
 
     nout = [0]
@@ -623,16 +643,12 @@ def rank_program(g, core, T, topo):
         wait("Y", deps("Y", [(buf, lo, hi)], []))
         g.sync.dma_start(dst, src).then_inc(T.sem.outs, 16)
         nout[0] += 16
-    landing(("KB4", 384, 512), "k", 3)
-    landing(("LW4", 384, 512), "l", 3)
     landing(("AR3", 0, 128), "s", 3)
-    mm(("VC", 0, 512), ("W08", 0, 8), ("KB4", 0, 512), True, True, mn=8)
-    act(("YU", 0, 512), ("VC", 0, 512), F.Copy, n=8)
-    act(("YL", 384, 512), ("LW4", 384, 512), F.Copy)
-    store(T.ylim[:], T.YL[:], "YL", 0, 512)
+    store(T.ylim[:, 0:384], T.YL[:, 0:384], "YL", 0, 384)
+    store(T.ylim[:, 384:512], T.YL[:, 384:512], "YL", 384, 512)
     store(T.yu[:], T.YU[:], "YU", 0, 512)
-    store(T.ysr[:, 0:256], T.SN[:], "SN", 0, 256)
     store(T.ysr[:, 256:384], T.DF[:], "DF", 0, 128)
+    store(T.ysr[:, 0:256], T.SN[:], "SN", 0, 256)
     store(T.ysr[:, 384:512], T.AR3[:], "AR3", 0, 128)
     g.wait_ge(T.sem.rloc, remote_total[0])
     g.wait_ge(T.sem.outs, nout[0])

from concourse.mybir import AluOpType as A, AxisListType, ActivationFunctionType as F

SCRATCH = {
    "FITW": ("sbuf", [128, 4096], "bfloat16"), "SRI": ("sbuf", [128, 512], "int32"), "LMI": ("sbuf", [128, 512], "int32"),
    "U8": ("sbuf", [8, 512], "int32"), "U16": ("sbuf", [8, 512], "float16"), "K8": ("sbuf", [8, 128], "bfloat16"),
    "E8A": ("sbuf", [8, 128], "bfloat16"), "E8": ("sbuf", [8, 128], "bfloat16"),
    "ON": ("sbuf", [128, 512], "bfloat16"), "ID": ("sbuf", [128, 128], "bfloat16"),
    "BLA": ("sbuf", [128, 128], "bfloat16"), "BLK": ("sbuf", [128, 128], "bfloat16"),
    "G8A": ("sbuf", [128, 8], "bfloat16"), "G8": ("sbuf", [128, 8], "bfloat16"), "LJ": ("sbuf", [128, 2048], "bfloat16"),
    "IOT": ("sbuf", [128, 512], "bfloat16"), "BI": ("sbuf", [128, 2], "int32"), "BJ": ("sbuf", [128, 2], "int32"),
    "BCF": ("sbuf", [128, 1], "float32"), "BCH": ("sbuf", [128, 1], "float32"),
    "JI": ("sbuf", [128, 96], "float32"), "M16": ("sbuf", [128, 96], "float32"), "TB": ("sbuf", [128, 144], "float32"),
    "TM": ("sbuf", [128, 96], "float32"), "COL": ("sbuf", [128, 8], "float32"), "W08": ("sbuf", [128, 8], "float16"),
    "R1": ("sbuf", [128, 8], "int32"), "R2": ("sbuf", [128, 8], "int32"), "R3": ("sbuf", [128, 8], "int32"),
    "R4": ("sbuf", [128, 8], "int32"), "RL": ("sbuf", [128, 8], "uint16"),
    "KI": ("sbuf", [128, 512], "int32"), "KJ": ("sbuf", [128, 512], "int32"),
    "SW": ("sbuf", [128, 512], "float32"), "SN": ("sbuf", [128, 256], "float32"),
    "SGV": ("sbuf", [128, 256], "float32"), "FN": ("sbuf", [128, 256], "bfloat16"), "WB": ("sbuf", [128, 256], "bfloat16"),
    "FL": ("sbuf", [128, 512], "bfloat16"), "CI": ("sbuf", [128, 512], "int32"), "CJ": ("sbuf", [128, 512], "int32"),
    "CRI": ("sbuf", [128, 256], "int32"), "CRJ": ("sbuf", [128, 256], "int32"),
    "CK": ("sbuf", [128, 512], "uint16"), "CR": ("sbuf", [128, 256], "uint16"),
    "LX": ("sbuf", [128, 8192], "bfloat16"), "CM": ("sbuf", [128, 8192], "bfloat16"), "CMR": ("sbuf", [128, 4096], "bfloat16"),
    "RS": ("sbuf", [128, 8192], "bfloat16"), "SG": ("sbuf", [128, 8192], "bfloat16"),
    "HH": ("sbuf", [128, 512], "bfloat16"), "OH": ("sbuf", [128, 512], "bfloat16"), "JUNK": ("sbuf", [128, 512], "bfloat16"),
    "ACC": ("sbuf", [128, 1], "float32"), "VAL": ("sbuf", [128, 512], "bfloat16"), "PR": ("sbuf", [128, 512], "bfloat16"),
    "PL": ("sbuf", [128, 32], "uint16"), "OI": ("sbuf", [128, 512], "bfloat16"), "OL": ("sbuf", [128, 32], "uint16"),
    "DM": ("sbuf", [128, 256], "float32"), "DFL": ("sbuf", [128, 128], "float32"), "DF": ("sbuf", [128, 128], "float32"),
    "YL": ("sbuf", [128, 512], "float32"), "YU": ("sbuf", [8, 512], "float32"),
}
for _w in ("N8", "P8", "N16", "P16", "NEG", "P4096"):
    SCRATCH["I_" + _w] = ("sbuf", [128, 128], "bfloat16")
for _t in range(4):
    SCRATCH["WT%d" % _t] = ("sbuf", [128, 128], "float16")
    SCRATCH["SO%d" % _t] = ("sbuf", [128, 512], "float32")
    SCRATCH["AR%d" % _t] = ("sbuf", [128, 128], "float32")
    SCRATCH["AW%d" % _t] = ("sbuf", [128, 128], "bfloat16")
    SCRATCH["KL%d" % _t] = ("sbuf", [128, 128], "bfloat16")
    SCRATCH["LL%d" % _t] = ("sbuf", [128, 128], "bfloat16")
    SCRATCH["WRV%d" % _t] = ("sbuf", [128, 256], "bfloat16")
for _t in range(5):
    SCRATCH["KB%d" % _t] = ("sbuf", [128, 512], "bfloat16")
    SCRATCH["LW%d" % _t] = ("sbuf", [128, 512], "bfloat16")
BANKS = ["D0", "D1", "OVV", "OVS", "GDA", "VA", "VB", "VC"]
for _b in BANKS:
    SCRATCH[_b] = ("psum", [128, 512], "float32")
SEMAPHORES = ["qV", "qS", "qT", "qG", "ldu", "lds", "ldl", "ldf", "outs", "rloc"]
SEMAPHORES += ["r%s%d" % (_k, _t) for _k in "sklw" for _t in range(4)]

CYC = 0.00083
GV, GS, SGN = 1.5 * CYC, 1.5 * CYC, 1.0 * CYC
VI, NV, NS = 320, 80, 64
VR = 180
V3 = 72


def rank_program(g, core, T, topo):
    rank = T.rank_of(core)
    if rank is None:
        return
    nxt = T.cores[(rank + 1) % len(T.cores)]
    assert topo.may_write(core, nxt)
    rid, pid = topo.addr(nxt)[:2]
    rmask = topo.mask(core, nxt)
    reng = len(topo.engines(core, nxt))
    Q = {"V": g.vector, "S": g.scalar, "T": g.tensor, "G": g, "Y": g.sync}
    cnt = {e: 0 for e in Q}
    known = {e: {} for e in Q}
    snaps = {}
    acc = {}
    ps = {b: ({}, {}) for b in BANKS}
    remote_total = [0]

    def wait(e, need):
        for s in sorted(need, key=lambda s: -len(snaps.get((s, need[s]), {}))):
            v = need[s]
            if known[e].get(s, 0) >= v:
                continue
            Q[e].wait_ge(T.sem[s], v)
            known[e][s] = v
            for s2, v2 in snaps.get((s, v), {}).items():
                if known[e].get(s2, 0) < v2:
                    known[e][s2] = v2

    def deps(e, R, W):
        need = {}

        def add(tok):
            if need.get(tok[0], 0) < tok[1]:
                need[tok[0]] = tok[1]
        for (b, lo, hi), w in [(x, False) for x in R] + [(x, True) for x in W]:
            if b in ps:
                anyd, wd = ps[b]
                for e2, c in anyd.items():
                    if e2 != e:
                        add(("q" + e2, c))
                if not w and e in wd:
                    add(("q" + e, wd[e]))
                continue
            for r in acc.get(b, ()):
                if r[0] < hi and lo < r[1]:
                    if not w and r[4]:
                        add(r[3])
                    elif w and r[2] != e:
                        add(r[3])
        return need

    def note(e, tok, R, W):
        for (b, lo, hi), w in [(x, False) for x in R] + [(x, True) for x in W]:
            if b in ps:
                ps[b][0][e] = tok[1]
                if w:
                    ps[b][1][e] = tok[1]
                continue
            L = acc.setdefault(b, [])
            if w:
                L[:] = [r for r in L if not (lo <= r[0] and r[1] <= hi)]
            else:
                L[:] = [r for r in L if not (not r[4] and r[2] == e and lo <= r[0] and r[1] <= hi)]
            L.append((lo, hi, e, tok, w))

    def op(e, fn, R=(), W=()):
        wait(e, deps(e, R, W))
        ins = fn(Q[e])
        cnt[e] += 1
        s = "q" + e
        ins.then_inc(T.sem[s], 1)
        snaps[(s, cnt[e])] = dict(known[e])
        note(e, (s, cnt[e]), R, W)

    def load(q, out, src, sem, buf, n):
        Q[q].dma_start(out, src).then_inc(T.sem[sem], 16)
        acc.setdefault(buf, []).append((0, n, "D", (sem, 16), True))

    def P(b, lo, hi, n=128):
        return T[b][0:n, lo:hi] if n < 128 else T[b][:, lo:hi]

    def cp(o, i):
        op("V", lambda q: q.tensor_copy(P(*o), P(*i)), [i], [o])

    def tt(o, a, b, f):
        op("V", lambda q: q.tensor_tensor(P(*o), P(*a), P(*b), f), [a, b], [o])

    def ts(o, a, s1, f1, s2=None, f2=None, n=128):
        R = [a]
        v1, v2 = s1, s2
        if isinstance(s1, tuple):
            R.append(s1)
            v1 = P(*s1)
        if isinstance(s2, tuple):
            R.append(s2)
            v2 = P(*s2)
        if f2 is None:
            op("V", lambda q: q.tensor_scalar(P(*o, n), P(*a, n), v1, None, f1), R, [o])
        else:
            op("V", lambda q: q.tensor_scalar(P(*o, n), P(*a, n), v1, v2, f1, f2), R, [o])

    def vgather(o, win, off):
        op("V", lambda q: q.tensor_copy(P(*o), P(*win).indirect(P(*off))), [win, off], [o])

    def sgather(o, win, off):
        op("S", lambda q: q.activation(P(*o), P(*win).indirect(P(*off)), F.Copy), [win, off], [o])

    def act(o, i, f, bias=0.0, scale=1.0, n=128):
        if f == F.Copy:
            op("S", lambda q: q.activation(P(*o, n), P(*i, n), f, scale=scale), [i], [o])
        else:
            op("S", lambda q: q.activation(P(*o, n), P(*i, n), f, bias=bias, scale=scale), [i], [o])

    def mm(o, lhs, rhs, start, stop, step=None, kn=128, mn=128):
        def f(q):
            r = T[rhs[0]][0:kn, rhs[1]:rhs[2]:step] if step else P(*rhs, kn)
            return q.matmul(P(*o, mn), P(*lhs, kn), r, start, stop)
        op("T", f, [lhs, rhs], [o])

    def lj(i):
        return ("LJ", i * 128, i * 128 + 128)

    def full(b):
        return (b, 0, 128)

    FW = ("FITW", 0, 4096)

    load("Y", T.U8[:], T.u[:], "ldu", "U8", 512)
    load("Y", T.SRI[:], T.sr[:], "lds", "SRI", 512)
    load("Y", T.LMI[:], T.lim[:], "ldl", "LMI", 512)
    load("S", T.FITW[:], T.fit[:], "ldf", "FITW", 4096)

    def sel(o, i, pat, cmp, base, cm, n=128):
        op("G", lambda q: q.affine_select(P(*o, n), P(*i, n), pat, cmp, 0.0, base, cm), [i], [o])

    def fill(o, v, n=128):
        op("V", lambda q: q.memset(P(*o, n), v), [], [o])
    fill(("ON", 0, 512), 1.0)
    fill(("K8", 0, 128), 256.0, 8)
    op("G", lambda q: q.iota(T.BI[:, 0:2], [[0, 2]], 0, 1), [], [("BI", 0, 2)])
    op("G", lambda q: q.iota(T.JI[:], [[0, 6], [1, 16]], 0, 0, allow_small_or_imprecise_dtypes=True), [], [("JI", 0, 96)])
    op("G", lambda q: q.iota(T.R1[:], [[0, 8]], 127, -1), [], [("R1", 0, 8)])
    op("G", lambda q: q.iota(T.R2[:], [[-16, 8]], 112, 0), [], [("R2", 0, 8)])
    sel(("E8A", 0, 128), ("ON", 0, 128), [[1, 128]], A.is_ge, 0, -16, 8)
    sel(("E8", 0, 128), ("E8A", 0, 128), [[-1, 128]], A.is_ge, 15, 16, 8)
    sel(("G8A", 0, 8), ("ON", 0, 8), [[-16, 8]], A.is_ge, 0, 1)
    sel(("G8", 0, 8), ("G8A", 0, 8), [[16, 8]], A.is_ge, 15, -1)
    sel(full("ID"), ("ON", 0, 128), [[-1, 128]], A.is_equal, 0, 1)
    sel(full("BLA"), ("ON", 0, 128), [[-16, 8], [0, 16]], A.is_ge, 0, 1)
    sel(full("BLK"), full("BLA"), [[16, 8], [0, 16]], A.is_ge, 15, -1)

    fill(("TB", 96, 112), 2.0)
    fill(("TB", 112, 128), 0.5)
    fill(("TB", 128, 144), 0.0)

    def scan(o, a, b, init, f0, f1):
        R = [a, b]
        iv = init
        if isinstance(init, tuple):
            R.append(init)
            iv = P(*init)
        op("V", lambda q: q.tensor_tensor_scan(P(*o), P(*a), P(*b), iv, f0, f1), R, [o])
    scan(("TB", 0, 16), ("TB", 112, 128), ("TB", 128, 144), 2.0, A.mult, A.add)
    for t in range(4):
        scan(("TB", 32 + 16 * t, 48 + 16 * t), ("TB", 96, 112), ("TB", 128, 144), 0.5, A.mult, A.add)
    ts(("BJ", 0, 2), ("BI", 0, 2), 15, A.bitwise_and)
    cp(("BCF", 0, 1), ("BJ", 0, 1))
    ts(("BCH", 0, 1), ("BCF", 0, 1), -0.5, A.add)
    ts(("M16", 0, 96), ("JI", 0, 96), ("BCF", 0, 1), A.is_equal)
    ts(("R3", 0, 8), ("R1", 0, 8), 15, A.bitwise_and)
    tt(("R4", 0, 8), ("R3", 0, 8), ("R2", 0, 8), A.add)
    cp(("RL", 0, 8), ("R4", 0, 8))

    ts(("U16", 0, 512), ("U8", 0, 512), -2048.0, A.add, n=8)
    cp(("LW0", 0, 512), ("LMI", 0, 512))
    mm(("VA", 0, 512), ("E8", 0, 128), ("U16", 0, 512), True, False, kn=8)
    mm(("VA", 0, 512), ("K8", 0, 128), ("ON", 0, 512), False, True, kn=8)

    def chain(s, v, o, x, y):
        return [lambda: tt(x, s, v, A.mult), lambda: ts(y, x, 5, A.logical_shift_right, 4095, A.bitwise_and), lambda: cp(o, y)]

    def cidx(*a):
        for f in chain(*a):
            f()
    cidx(("SRI", 0, 512), ("VA", 0, 512), ("CK", 0, 512), ("CI", 0, 512), ("CJ", 0, 512))
    ts(("FL", 0, 512), ("SRI", 0, 512), 4096.0, A.is_ge)

    def expand(L, a0, a1, i, e="V"):
        o = T.LX[:, a0 * 16 + i:a1 * 16:16]
        if e == "V":
            op("V", lambda q: q.tensor_copy(o, P(L, a0, a1)), [(L, a0, a1)], [("LX", a0 * 16, a1 * 16)])
        elif e == "G":
            op("G", lambda q: q.affine_select(o, P(L, a0, a1), [[1, a1 - a0]], A.is_ge, 0.0, 0, 0), [(L, a0, a1)], [("LX9", a0 * 16, a1 * 16)])
        else:
            op("S", lambda q: q.activation(o, P(L, a0, a1), F.Copy), [(L, a0, a1)], [("LX8", a0 * 16, a1 * 16)])
    for i in range(4):
        act(("LJ", 512 * i, 512 * i + 512), ("ON", 0, 512), F.Copy, scale=0.0)
    wait("S", {"qS": cnt["S"]})
    for i in range(16):
        o = T.LJ[:, i * 128 + i:(i + 1) * 128:16]
        op("S", lambda q: q.activation(o, T.G8[:], F.Copy), [("G8", 0, 8)], [lj(i)])
    for k, v in (("NEG", -1.0), ("N8", -8.0), ("P8", 8.0), ("N16", -16.0), ("P16", 16.0), ("P4096", 4096.0)):
        act(full("I_" + k), full("ID"), F.Copy, scale=v)
    for i in range(5):
        expand("LW0", 0, VI, i, "S")
    for i in range(5, 10):
        expand("LW0", 0, VI, i, "G")
    for i in range(10, 16):
        expand("LW0", 0, VI, i)

    def gfill(lo, hi, v):
        op("G", lambda q: q.affine_select(P("TB", lo, hi), P("JI", 0, hi - lo), [[0, hi - lo]], A.is_gt, v, 0, 0), [("JI", 0, 16)], [("TB", lo, hi)])
    eps = -0.5 + 2.0 ** -13
    gfill(17, 28, eps)
    for j, v in ((16, -0.25), (28, 997 / 4096 + eps), (29, 1994 / 4096 + eps), (30, 5200 / 4096 + eps), (31, 1.0)):
        gfill(j, j + 1, v)
    gfill(12, 14, 2.0 ** -12)
    gfill(14, 15, -2.0 ** -12)
    gfill(15, 16, 0.0)
    gfill(44, 48, 0.0)
    for t, w in ((1, (-4096.0, 0.0, 0.0, 997.0)), (2, (0.0, -4096.0, 0.0, 1994.0)), (3, (0.0, 0.0, 4096.0, -1105.0))):
        for j in range(4):
            gfill(44 + 16 * t + j, 45 + 16 * t + j, w[j])
    op("G", lambda q: q.iota(T.IOT[:], [[1, 512]], -256, 0, allow_small_or_imprecise_dtypes=True), [], [("IOT", 0, 512)])

    def columns():
        tt(("TM", 0, 96), ("TB", 0, 96), ("M16", 0, 96), A.mult)
        for k in range(6):
            op("V", lambda q: q.tensor_reduce(P("COL", k, k + 1), P("TM", 16 * k, 16 * k + 16), AxisListType.X, A.add),
               [("TM", 16 * k, 16 * k + 16)], [("COL", k, k + 1)])
        weights(0)

    def weights(t0):
        for t in (t0, t0 + 1):
            ts(full("WT%d" % t), full("BLK"), ("COL", 2 + t, 3 + t), A.mult)
        if t0:
            ts(("W08", 0, 8), ("G8", 0, 8), ("COL", 2, 3), A.mult)

    def vcmp(out, lst, a0, n):
        o, x, l = (out, a0 * 16, (a0 + n) * 16), ("LX", a0 * 16, (a0 + n) * 16), (lst, a0, a0 + n)
        op("V", lambda q: q.tensor_tensor(P(*o), P(*FW).indirect(P(*l)), P(*x), A.is_gt),
           [FW, l, x, ("LX8", a0 * 16, (a0 + n) * 16), ("LX9", a0 * 16, (a0 + n) * 16)], [o])

    def vcount(src, a0, n, dst, d0, extra):
        for i in range(16):
            mm((dst, d0, d0 + n), lj(i), (src, a0 * 16 + i, (a0 + n) * 16), i == 0, False, step=16)
        ends(dst, d0, n, extra)

    def ends(dst, d0, n, extra):
        for k, (w, r) in enumerate(extra):
            mm((dst, d0, d0 + n), full("I_" + w), r, False, k == len(extra) - 1)

    def sgat(lst, a0, n):
        sgather(("RS", a0 * 16, (a0 + n) * 16), FW, (lst, a0, a0 + n))

    def sdiff(L, a0, n, h):
        for k in range(8):
            d = ("D%d" % h, k * n, k * n + n)
            mm(d, full("I_NEG"), (L, a0, a0 + n), True, False)
            mm(d, full("ID"), ("RS", a0 * 16 + 8 * h + k, (a0 + n) * 16), False, True, step=16)

    def ssign(a0, n, h):
        act(("SG", a0 * 16 + 8 * h * n, a0 * 16 + 8 * h * n + 8 * n), ("D%d" % h, 0, 8 * n), F.Sign, bias=-0.5)

    def scount(a0, n, dst, d0, extra):
        for i in range(16):
            mm((dst, d0, d0 + n), lj(i), ("SG", a0 * 16 + i * n, a0 * 16 + (i + 1) * n), i == 0, False)
        ends(dst, d0, n, extra)

    def schunks(chunks):
        prev = None
        for ch in list(chunks) + [None]:
            if ch is not None:
                if ch[0]:
                    if prev is not None and ch[0] not in events:
                        for y in sfin(prev):
                            yield y
                        prev = None
                    yield ch[0]
                sgat(ch[1], ch[3], ch[4])
                yield 16 * ch[4] * GS
                for h in (0, 1):
                    if prev is not None:
                        ssign(prev[3], prev[4], h)
                        yield 8 * prev[4] * SGN
                    sdiff(ch[2], ch[3], ch[4], h)
                if prev is not None:
                    prev[5]()
                    yield ("set", "sg%d" % prev[3])
                prev = ch
            elif prev is not None:
                for y in sfin(prev):
                    yield y

    def sfin(ch):
        for h in (0, 1):
            ssign(ch[3], ch[4], h)
            yield 8 * ch[4] * SGN
        ch[5]()
        yield ("set", "sg%d" % ch[3])

    events = {}

    def run(streams):
        events.clear()
        L = [[s, 0.0, None] for s in streams]
        while L:
            ok = [x for x in L if x[2] is None or x[2] in events]
            assert ok, [x[2] for x in L]
            x = min(ok, key=lambda x: max(x[1], events.get(x[2], 0.0)))
            if x[2] is not None:
                x[1] = max(x[1], events[x[2]])
                x[2] = None
            try:
                y = next(x[0])
            except StopIteration:
                L.remove(x)
                continue
            if isinstance(y, str):
                x[2] = y
            elif isinstance(y, tuple):
                events[y[1]] = x[1]
            else:
                x[1] += y

    def send(dst, src, sem, t):
        b, lo, hi = src
        wait("G", deps("G", [src], []))
        g.remote_dma(P(*dst), P(b, lo, hi), T.sem["r%s%d" % (sem, t)], T.sem.rloc, pid, rid, rmask)
        remote_total[0] += reng

    def landing(dst, sem, t):
        acc.setdefault(dst[0], []).append((dst[1], dst[2], "D", ("r%s%d" % (sem, t), reng), True))

    def order(hspec, sregs, t):
        first = t == 0
        for bank, a0, a1, thr in hspec:
            if isinstance(thr, tuple):
                tt(("HH", a0, a1), (bank, a0, a1), thr, A.is_ge)
            else:
                ts(("HH", a0, a1), (bank, a0, a1), thr, A.is_ge)
            mm(("VC", a0, a1), full("BLK"), ("HH", a0, a1), True, True)
            mm(("VB", a0, a1), full("BLK"), ("HH", a0, a1), True, True)
        hh, vb, vc = ("HH", 0, 512), ("VB", 0, 512), ("VC", 0, 512)
        mm(("D0", 0, 512), full("I_P4096"), hh, True, True)
        if first:
            ts(("KI", 0, 512), ("VA", 0, 512), ("COL", 0, 1), A.mult, ("COL", 1, 2), A.add)
        ts(("OH", 0, 512), vb, 15.0, A.min, ("BCF", 0, 1), A.is_equal)
        op("S", lambda q: q.activation(T.JUNK[:], P(*vc), F.Sign, bias=T.BCH[:], scale=-1.0, accum_out=T.ACC[:]),
           [vc, ("BCH", 0, 1)], [("JUNK", 0, 512), ("ACC", 0, 1)])
        mm(("GDA", 0, 512), full("ID"), ("OH", 0, 512), True, True)
        if first:
            ts(("KJ", 0, 512), ("KI", 0, 512), 1, A.bitwise_and)
        scan(("VAL", 0, 512), ("OH", 0, 512), ("OH", 0, 512), ("ACC", 0, 1), A.add, A.add)
        tt(("PR", 0, 512), ("VAL", 0, 512), ("GDA", 0, 512), A.mult)
        for j in range(16):
            mm(("D1", 0, 32), lj(j), ("PR", j, 512), j == 0, j == 15, step=16)
        for (b, lo, hi), a0 in sregs:
            tt(("SW", a0, a0 + hi - lo), (b, lo, hi), ("D0", a0, a0 + hi - lo), A.max)
        ts(("PL", 0, 32), ("D1", 0, 32), 0.5, A.mult, 255.0, A.add)
        op("V", lambda q: q.tensor_copy(T.OI[:].indirect(T.PL[:]), T.IOT[:]), [("PL", 0, 32), ("IOT", 0, 512)], [("OI", 0, 512)])
        if first:
            cp(("KB0", 0, 512), ("KJ", 0, 512))
        if t == 1:
            weights(2)
        for j in range(16):
            mm(("D1", 0, 32), lj(j), ("OI", j, 512), j == 0, j == 15, step=16)
        ts(("OL", 0, 32), ("D1", 0, 32), 0.0625, A.mult, 256.0, A.add)

    def v_first():
        for a0 in range(0, VI, NV):
            vcmp("CM", "CK", a0, NV)
            if a0 + NV == VI:
                columns()
            yield 16 * NV * GV
            vcount("CM", a0, NV, "OVV", a0, [("P16", ("FL", a0, a0 + NV))])

    def s_first():
        def fin(a0):
            return lambda: scount(a0, NS, "OVS", a0, [("P16", ("FL", a0, a0 + NS))] * 2)
        for y in schunks([(None, "CK", "LW0", a0, NS, fin(a0)) for a0 in range(VI, 512, NS)]):
            yield y
    run([v_first(), s_first()])
    hspec = [("OVV", 0, VI, 11.5), ("OVS", VI, 512, 7.0)]
    sregs = [(("SRI", 0, 512), 0)]

    for t in range(4):
        last = t == 3
        order(hspec, sregs, t)
        SO, KB, LW, KL, LL, AR, AW, WRV = ["%s%d" % (k, n) for k, n in (("SO", t), ("KB", t + 1), ("LW", t + 1), ("KL", t), ("LL", t), ("AR", t), ("AW", t), ("WRV", t))]
        KO, LO = "KB%d" % t, "LW%d" % t
        VS = 128 + V3 if last else VR
        VA3 = V3 if last else 128
        NR = (256 - VS) // 2

        def rob(a0, n):
            d, d0 = ("GDA", a0) if a0 < 128 else ("VB", a0 - 128)
            vcount("CMR", a0, n, d, d0, [("N8", ("FL", a0, a0 + n))])

        def finish(h0, final=None, so=None):
            d = "GDA" if h0 == 0 else "VB"
            k = VS - 128 if h0 else VA3
            ts(("WB", h0, h0 + k), (d, 0, k), -0.5, A.is_ge, 8192.0, A.mult)
            if k < 128:
                ts(("WB", h0 + k, h0 + 128), (d, k, 128), -17.0, A.is_ge, 8192.0, A.mult)
            if final:
                op("V", lambda q: q.tensor_scalar(T.DM[:, h0:h0 + 128], T.WB[:, h0:h0 + 128].indirect(T.RL[:]), -0.5, 4096.0, A.mult, A.add),
                   [("WB", h0, h0 + 128), ("RL", 0, 8)], [("DM", h0, h0 + 128)])
                tt((final, 0, 128), so, ("DM", h0, h0 + 128), A.max)
                if h0 == 0:
                    send((AR, 0, 128), (final, 0, 128), "s", t)
            tt((d, 256, 384), ("SGV", h0, h0 + 128), ("WB", h0, h0 + 128), A.max)
            tt(("SN", h0, h0 + 128), (SO, h0, h0 + 128), (d, 256, 384), A.min)

        def recv_list(h0):
            cidx(("SN", h0, h0 + 128), ("VA", h0, h0 + 128), ("CK", h0, h0 + 128), ("CI", h0, h0 + 128), ("CJ", h0, h0 + 128))

        def chk(a0, n):
            vcount("CM", a0, n, "OVV", a0, [("P8", ("FN", a0, a0 + n))])

        def v_round():
            vgather((SO, 256, 512), ("SW", 0, 512), ("OL", 16, 32))
            if not last:
                send((AR, 0, 128), (SO, 384, 512), "s", t)
            yield 256 * GV
            vgather((SO, 0, 256), ("SW", 0, 512), ("OL", 0, 16))
            yield ("set", "SO")
            yield 256 * GV
            yield "v"
            if last:
                vgather(("SGV", 0, 128), (SO, 384, 512), ("RL", 0, 8))
                cidx(("SGV", 0, 128), ("VB", 0, 128), ("CR", 0, 128), ("CRI", 0, 128), ("CRJ", 0, 128))
                yield 0.55
            else:
                cD = chain((SO, 256, 384), ("VA", 256, 384), ("CK", 256, 384), ("CI", 256, 384), ("CJ", 256, 384))
                cD[0]()
                vgather(("SGV", 0, 128), (SO, 384, 512), ("RL", 0, 8))
                cD[1]()
                vgather(("SGV", 128, 256), (SO, 256, 384), ("RL", 0, 8))
                cD[2]()
                yield 256 * GV + 0.35
                yield ("set", "cD")
                cidx(("SGV", 0, 256), ("VB", 0, 256), ("CR", 0, 256), ("CRI", 0, 256), ("CRJ", 0, 256))
                yield 0.65
            yield ("set", "cR")
            yield "lim"
            for i in range(16):
                expand(LW, 0, VA3, i)
            yield 0.85
            yield "FL"
            for a0, n in ((0, V3),) if last else ((0, 64), (64, 64)):
                vcmp("CMR", "CR", a0, n)
                yield 16 * n * GV * (0.3 if a0 == 64 else 1)
                if a0 == 64:
                    landing((AR, 0, 128), "s", t)
                    landing((KB, 384, 512), "k", t)
                    landing((LW, 384, 512), "l", t)
                    mm(("VC", 0, 128), full("WT%d" % (t + 1)), (KB, 384, 512), True, True)
                    yield 16 * n * GV * 0.7
                rob(a0, n)
            if last:
                vgather(("SGV", 128, 256), (SO, 256, 384), ("RL", 0, 8))
                cidx(("SGV", 128, 256), ("VB", 128, 256), ("CR", 128, 256), ("CRI", 128, 256), ("CRJ", 128, 256))
                yield ("set", "cRB")
                yield "sg%d" % V3
                finish(0, "DFL", (SO, 384, 512))
                yield 0.9
                yield "LXB"
                vcmp("CMR", "CR", 128, V3)
                yield 16 * V3 * GV
                rob(128, V3)
                yield "sg%d" % VS
                finish(128, "DF", (SO, 256, 384))
                return
            cidx((AR, 0, 128), ("VC", 0, 128), ("CK", 384, 512), ("CI", 384, 512), ("CJ", 384, 512))
            yield 0.35
            yield ("set", "cArr")
            yield "LXB"
            vcmp("CMR", "CR", 128, VS - 128)
            yield 16 * (VS - 128) * GV
            rob(128, VS - 128)
            finish(0)
            yield 0.55
            recv_list(0)
            yield 0.4
            yield ("set", "wA")
            for a0 in (0, 64, 128, 192):
                if a0 == 128:
                    yield "sg%d" % (256 - NR)
                    finish(128)
                    recv_list(128)
                    yield 0.9
                    yield ("set", "wB")
                vcmp("CM", "CK", a0, 64)
                yield 1024 * GV
                yield "rB" if a0 >= 128 else "rA"
                chk(a0, 64)

        def rev(h0):
            o = 128 - h0
            op("S", lambda q: q.activation(P(WRV, o, o + 128), T.WB[:, h0:h0 + 128].indirect(T.RL[:]), F.Identity, bias=-41.0, scale=2.0 ** -8),
               [("WB", h0, h0 + 128), ("RL", 0, 8)], [(WRV, o, o + 128)])
            if h0 == 0:
                send((AW, 0, 128), (WRV, 128, 256), "w", t)
            act(("FN", h0, h0 + 128), ("SN", h0, h0 + 128), F.Sign, bias=-4095.5)

        def s_round():
            sgather((KB, 0, 384), (KO, 0, 512), ("OL", 0, 24))
            if not last:
                mm(("VA", 0, 384), full("WT%d" % (t + 1)), (KB, 0, 384), True, True)
            mm(("VB", 0, 256), full("WT%d" % t), (KB, 0, 256), True, True)
            yield 384 * GS
            yield ("set", "v")
            sgather((KL, 0, 128), (KO, 0, 512), ("OL", 24, 32))
            send((KB, 384, 512), (KL, 0, 128), "k", t)
            yield 128 * GS
            sgather((LW, 0, 384), (LO, 0, 512), ("OL", 0, 24))
            yield 384 * GS
            yield ("set", "lim")
            sgather((LL, 0, 128), (LO, 0, 512), ("OL", 24, 32))
            send((LW, 384, 512), (LL, 0, 128), "l", t)
            yield 128 * GS
            for i in range(16):
                expand(LW, 128, VS, i, "G")
            yield ("set", "LXB")
            if not last:
                for i in range(16):
                    expand(LW, VS, 256, i, "G")
            yield "SO"
            act(("FL", 0, 384), (SO, 0, 384), F.Sign, bias=-4095.5)
            yield 384 * CYC
            yield ("set", "FL")
            if last:
                n = 128 - V3
                yield "cR"
                for a0, d in ((V3, "GDA"), (VS, "VB")):
                    if d == "VB":
                        yield "cRB"
                    sgat("CR", a0, n)
                    yield 16 * n * GS
                    sdiff(LW, a0, n, 0)
                    sdiff(LW, a0, n, 1)
                    if d == "GDA":
                        act(("YL", 0, 384), (LW, 0, 384), F.Copy)
                        yield 384 * CYC
                    for y in sfin((None, None, None, a0, n, lambda: scount(a0, n, d, V3, [("N16", ("FL", a0, a0 + n))]))):
                        yield y
                landing(("KB4", 384, 512), "k", 3)
                landing(("LW4", 384, 512), "l", 3)
                mm(("VC", 0, 512), ("W08", 0, 8), ("KB4", 0, 512), True, True, mn=8)
                act(("YU", 0, 512), ("VC", 0, 512), F.Copy, n=8)
                act(("YL", 384, 512), ("LW4", 384, 512), F.Copy)
                return

            def don(a0):
                return lambda: scount(a0, 64, "OVS", a0, [("P16", ("FL", a0, a0 + 64))])

            def robs(a0):
                return lambda: scount(a0, NR, "VB", a0 - 128, [("N16", ("FL", a0, a0 + NR))])

            def arr():
                act(("FL", 384, 512), (AR, 0, 128), F.Sign, bias=-4095.5)
                don(384)()
            for y in schunks([("cD", "CK", LW, 256, 64, don(256)),
                              ("cR", "CR", LW, VS, NR, robs(VS)), ("cR", "CR", LW, VS + NR, NR, robs(VS + NR)),
                              (None, "CK", LW, 320, 64, don(320)), ("cArr", "CK", LW, 384, 64, arr), (None, "CK", LW, 448, 64, don(448))]):
                yield y

        def s_rev():
            yield "wA"
            rev(0)
            yield 128 * GS
            yield ("set", "rA")
            yield "wB"
            rev(128)
            yield 128 * GS
            yield ("set", "rB")

        run([v_round(), s_round()] + ([] if last else [s_rev()]))
        if not last:
            landing((AW, 0, 128), "w", t)
            hspec = [("OVS", 256, 384, (WRV, 0, 128)), ("OVS", 384, 512, (AW, 0, 128)), ("OVV", 0, 256, 3.5)]
            sregs = [(("SN", 0, 256), 0), ((SO, 256, 384), 256), ((AR, 0, 128), 384)]

    nout = [0]

    def store(dst, src, buf, lo, hi):
        wait("Y", deps("Y", [(buf, lo, hi)], []))
        g.sync.dma_start(dst, src).then_inc(T.sem.outs, 16)
        nout[0] += 16
    landing(("AR3", 0, 128), "s", 3)
    store(T.ylim[:, 0:384], T.YL[:, 0:384], "YL", 0, 384)
    store(T.ylim[:, 384:512], T.YL[:, 384:512], "YL", 384, 512)
    store(T.yu[:], T.YU[:], "YU", 0, 512)
    store(T.ysr[:, 256:384], T.DF[:], "DF", 0, 128)
    store(T.ysr[:, 0:256], T.SN[:], "SN", 0, 256)
    store(T.ysr[:, 384:512], T.AR3[:], "AR3", 0, 128)
    g.wait_ge(T.sem.rloc, remote_total[0])
    g.wait_ge(T.sem.outs, nout[0])
    for e in "VSTG":
        g.wait_ge(T.sem["q" + e], cnt[e])
